import numpy as np, ml_dtypes
CORES = [48,51,52,55]
N = 4
import mx_ref
BF = ml_dtypes.bfloat16
def gcols(t, e):
    v = np.concatenate([t.reshape(8, 16, -1, 4), np.zeros((8, 16, 1, 4), BF)], axis=2)
    return np.ascontiguousarray(np.stack([v[g][:, e[g]] for g in range(8)])).reshape(128, -1)
def tile(rs):
    return np.stack(rs, axis=2).reshape(128, -1).astype(BF)
def cut(t, i, w=512):
    return t[:, w * i:w * i + w]
def pick(q, e):
    c = np.concatenate([q[0].reshape(128, -1, 4), np.zeros((128, 1, 4), np.uint8)], axis=1); s = np.concatenate([q[1], np.ones((16, 1), np.uint8)], axis=1)
    return (np.ascontiguousarray(c[:, e].reshape(128, -1)), np.ascontiguousarray(s[:, e]))
def join(*qs):
    return (np.concatenate([q[0] for q in qs], axis=1), np.concatenate([q[1] for q in qs], axis=1))
def put(q, e, v):
    c, s = q[0].reshape(128, -1, 4).copy(), q[1].copy(); c[:, e] = v[0].reshape(128, -1, 4); s[:, e] = v[1]
    return (c.reshape(128, -1), s)
def pk(c, s):
    return (np.ascontiguousarray(c), mx_ref.live(s))
def emit(q):
    return q[0], q[1]
def packed(v, rng):
    q = [mx_ref.quantize(np.ascontiguousarray(v[r])) for r in range(N)]
    return np.stack([a for a, b in q]), np.stack([mx_ref.plane(b, rng) for a, b in q])
def values_of_codes():
    e, c = np.zeros((128, 128, 4), np.float32), np.zeros((128, 2, 4), np.uint8)
    e[np.arange(128), np.arange(128), 0] = 1
    c[:127, :, 0] = np.arange(256).reshape(2, 128).T[:127]
    return mx_ref.matmul(mx_ref.quantize(e.reshape(128, 512).astype(BF)), (c.reshape(128, 8), np.full((16, 2), 127, np.uint8))).T.reshape(-1).astype(np.float64)
CODE_VALUE, SCALE_VALUE = values_of_codes(), 2.0 ** (np.arange(256) - 127.0)
def decode(q):
    return (CODE_VALUE[q[0]].reshape(16, 8, -1, 4) * SCALE_VALUE[q[1]][:, None, :, None] + 0.0).reshape(128, -1).astype(np.float32)
def f(rng, *shape):
    return mx_ref.flush((rng.standard_normal(shape, dtype=np.float32) * np.exp2(rng.integers(-2, 3, shape[:-1] + (1,)))).astype(BF))
def wide(rng, *shape, cols=0):
    v = rng.standard_normal(shape, dtype=np.float32) * np.exp2(rng.integers(-12, 13, shape)).astype(np.float32)
    if cols: v *= np.repeat(np.exp2(rng.integers(-cols, cols + 1, shape[:-2] + (1, shape[-1] // 4))) * (rng.random(shape[:-2] + (1, shape[-1] // 4)) > 0.0625), 4, axis=-1).astype(np.float32)
    return mx_ref.flush(v.astype(BF))
C, S, R = 384, 96, 2
STEP = [2, 1]
def partner(r, t):
    return r ^ STEP[t]
def order(p):
    return np.argsort(-(p[::16] + np.float32(0.0)), axis=1, kind="stable")
def walk(pi):
    g, p = np.arange(8), np.zeros(8, int)
    e, taken = np.zeros((8, C), int), np.zeros((8, C), bool)
    for k in range(C):
        e[:, k] = p
        taken[g, p] = True
        p = pi[g, p]
        p = np.where(taken[g, p], np.argmin(taken, axis=1), p)
    return e
def common(w, rng):
    c, p = packed(np.stack([w] * N), rng)
    return {"wc": c, "ws": p}
def weights(rng, keep=()):
    w = np.array(f(rng, 128, 2048)).reshape(128, 4, 8, 16, 4)
    for p in keep: w[:, :, :, p] = 0
    if len(keep): w[::16] = 0
    return common(w.reshape(128, 2048), rng)
def numbers_of(rng):
    return {"x": np.array(f(rng, N, 128, 4 * C)), "u": np.stack([f(rng, 128, 512)] * N), "v": np.array(f(rng, N, 128, 512))}
def planted(rng, s, sign, kind):
    d = numbers_of(rng)
    x = d["x"].astype(np.float32).reshape(N, 8, 16, C, 4)
    digit = ((s[:, :, :, None] >> np.arange(12)) & 1) * np.exp2(np.arange(12) - 23.0)
    x[:, :, 0] = 0
    x[:, :, 0, :, 0] = sign[:, :, None]
    for a in range(3): x[:, :, 8 + a] = digit[:, :, :, 4 * a:4 * a + 4]
    x[:, :, 11:] = rng.integers(4, 8, (N, 8, 5, C, 4)) * rng.choice([-1.0, 1.0], (N, 8, 5, C, 4)) * 2.0 ** -20
    u = d["u"].reshape(N, 128, 128, 4)
    u[:, :, ::16] = 0
    for g in range(8):
        k = 1.0 if kind[g] < 2 else 2.0 ** -30
        u[:, 16 * g, 16 * g, 0] = k
        u[:, 16 * g + 8:16 * g + 11, 16 * g] = k
        if kind[g] == 1: x[:, g, 0, int(rng.integers(C)), 0] *= 2.0 ** 30
        if kind[g] == 3:
            x[:, g, 0] = 0
            x[:, g, 8:] *= 2.0 ** -7
            x[:, g, 8:11] *= sign[:, g][:, None, None, None]
            x[:, g, 11] = 0
            u[:, 16 * g + 11, 16 * g, 0] = 1.125 * k
            u[:, 16 * g + 11, 16 * g, 1] = k
            for r in range(N):
                if r & STEP[0]:
                    j = int(np.flatnonzero(s[r, g] == 0)[-1])
                    x[r, g, 11, j, 0] = 1.125 * 2.0 ** -30
                    x[r, g, 11, j, 1] = -1.25 * 2.0 ** -30
    return {"x": x.reshape(N, 128, 4 * C).astype(BF), "u": u.reshape(N, 128, 512), "v": d["v"], **weights(rng, [0] + [*range(8, 16)])}
def setup_inputs(rng):
    return {**numbers_of(rng), **weights(rng)}
def setup_inputs_ties(rng):
    d = numbers_of(rng)
    e = rng.permutation(N)
    x = d["x"].reshape(N, 8, 16, C, 4)
    for r in range(N):
        for g in range(8):
            k = np.zeros(C, int) if r == e[0] else rng.permutation(C) % 3
            a = x[r, g, :8, :3].copy()
            a[:, 2] = 0
            x[r, g, :8] = a[:, k]
    x[e[1]] = 0
    u = d["u"].reshape(N, 8, 16, 128, 4)
    for g in range(8):
        own = u[:, g, :8, 16 * g].copy()
        u[:, :, :, 16 * g] = 0
        u[:, g, :8, 16 * g] = own
    return {"x": x.reshape(N, 128, 4 * C), "u": u.reshape(N, 128, 512), "v": d["v"], **weights(rng, [*range(8)])}
def setup_inputs_near(rng):
    s = np.stack([np.stack([rng.permutation(C) // 2 for g in range(8)]) for r in range(N)])
    sign = np.stack([rng.permutation(8) % 2 * 2.0 - 1.0 for r in range(N)])
    return planted(rng, s, sign, rng.permutation(8) % 4)
def setup_inputs_cycles(rng):
    size = [[C], [257] + [1] * (C - 257), [2] * (C // 2), [3] * (C // 3) + [1] * (C % 3)]
    s = np.zeros((N, 8, C), int)
    h = rng.permutation(8)
    for q in range(N):
        if q & (STEP[0] | STEP[1]): continue
        for g in range(8):
            i, m, pi, at = rng.permutation(C), rng.permutation(C), np.zeros(C, int), 0
            if h[g] // 2 == 0:
                m = np.roll(m, -int(np.argmin(m)))
                m[1:3] = np.sort(m[1:3])
                m[-2:] = np.sort(m[-2:])[::-1]
            for n in size[h[g] // 2]:
                pi[m[at:at + n]] = np.roll(m[at:at + n], -1)
                at += n
            other = i.copy()
            if h[g] == 4:
                k = pi[np.flatnonzero(pi > np.arange(C))[-2:]]
                other[k] = i[k[::-1]]
            for r in (q, q ^ STEP[0], q ^ STEP[1], q ^ STEP[0] ^ STEP[1]):
                c = other if r & STEP[1] else i
                s[r, g] = C - 1 - (c[pi] if r & STEP[h[g] % 2] else c)
    sign = np.tile(rng.permutation(8) % 2 * 2.0 - 1.0, (N, 1))
    return planted(rng, s, sign, rng.permutation(8) % 2 * 2)
def setup_inputs_huge(rng):
    d = numbers_of(rng)
    x = 2.0 ** 30 * (0.9 + 0.1 * rng.random((N, 128, C, 4)))
    x[:, ::8, :, 0] = 2.0 ** 30
    c = np.stack([rng.permutation(C) % 2 * 2.0 - 1.0 for r in range(N)])
    c[rng.permutation(N) < N // 2] = 1
    x *= c[:, None, :, None]
    u = d["u"].reshape(N, 128, 128, 4)
    a = 2.0 ** 30 * (1 - 0.1 * rng.random((128, 8, 4))) * (rng.permutation(8) % 2 * 2.0 - 1.0)[None, :, None]
    u[:, :, ::16] = a.astype(np.float32).astype(BF)
    w = np.zeros((128, 4, 128, 4), np.float32)
    i = np.arange(128)
    for b in range(4): w[i, b, i, b] = -8
    return {"x": x.astype(np.float32).reshape(N, 128, 4 * C).astype(BF), "u": u.reshape(N, 128, 512), "v": d["v"], **common(w.reshape(128, 2048).astype(BF), rng)}
def setup_inputs_spread(rng):
    d = setup_inputs(rng)
    d["x"] = wide(rng, N, 128, 4 * C, cols=6)
    return d
def check_inputs(d):
    b = []
    for k in ("x", "u", "v"):
        a = np.abs(d[k].astype(np.float32))
        if not (np.isfinite(a).all() and ((a == 0) | (a >= 2.0 ** -30) & (a <= 2.0 ** 30)).all()): b.append("a value of " + k)
    if (d["u"].astype(np.float32) != d["u"][:1].astype(np.float32)).any(): b.append("u differs between ranks")
    if (d["wc"] % 128 == 127).any(): b.append("a code of wc is no number")
    if (d["wc"] != d["wc"][:1]).any(): b.append("wc differs between ranks")
    s = [mx_ref.live(p) for p in d["ws"]]
    if any((p != s[0]).any() for p in s): b.append("ws differs between ranks")
    return b
def reference(x, u, v, wc, ws):
    w, qu = pk(wc[0], ws[0]), mx_ref.quantize(u[0])
    now = [x[r] for r in range(N)]
    for t in range(R):
        o = [order(mx_ref.matmul(qu, mx_ref.quantize(now[r]))) for r in range(N)]
        i = [np.argsort(o[r], axis=1) for r in range(N)]
        e = [walk(np.take_along_axis(o[r], i[partner(r, t)], axis=1)) for r in range(N)]
        laid = [gcols(now[r], e[r]) for r in range(N)]
        came = decode(join(*[mx_ref.quantize(np.ascontiguousarray(laid[r][:, :4 * S])) for r in range(N)])).astype(BF)
        for r in range(N):
            z = np.ascontiguousarray(np.concatenate([cut(came, partner(r, t), 4 * S), laid[r][:, 4 * S:]], axis=1))
            q = mx_ref.quantize(z)
            now[r] = tile([z[:, b::4].astype(np.float32) + mx_ref.matmul(pick(w, np.arange(128 * b, 128 * b + 128)), q) * np.float32(0.015625) for b in range(4)])
    y, el = np.zeros((N, 128, C), np.float32), np.zeros((N, 8, C), np.float32)
    oc, osc = np.zeros((N, 128, 4 * C), np.uint8), np.zeros((N, 16, C), np.uint8)
    for r in range(N):
        q = mx_ref.quantize(now[r])
        y[r] = mx_ref.matmul(mx_ref.quantize(v[r]), q)
        el[r] = e[r]
        oc[r], osc[r] = emit(q)
    return {"y": y, "el": el, "oc": oc, "osc": osc}

@@ -1,0 +1,382 @@
+from concourse.mybir import dt, AluOpType, ActivationFunctionType
+
+ALU = AluOpType
+ACT = ActivationFunctionType
+C, S, R = 384, 96, 2
+STEP = [2, 1]
+NW = C // 16
+NV = 15
+BIG = 2.0 ** 40
+MAGIC = 12582912.0
+H = C // 2
+X4, U8, BF, F32, U16, I32 = "float8_e4m3fn_x4", "uint8", "bfloat16", "float32", "uint16", "int32"
+
+SCRATCH = {
+    "ps": ("psum", [128, 4096], F32),
+    "ut": ("sbuf", [128, 512], BF), "vt": ("sbuf", [128, 512], BF),
+    "qu": ("sbuf", [128, 128], X4), "su": ("sbuf", [128, 128], U8),
+    "qur": ("sbuf", [128, 128], X4), "sur": ("sbuf", [128, 128], U8),
+    "qv": ("sbuf", [128, 128], X4), "sv": ("sbuf", [128, 128], U8),
+    "qw": ("sbuf", [128, 512], X4), "sw": ("sbuf", [128, 512], U8),
+    "ones": ("sbuf", [128, 528], BF), "et": ("sbuf", [128, 528], BF),
+    "qe": ("sbuf", [128, 512], X4), "se": ("sbuf", [128, 512], U8),
+    "ci": ("sbuf", [128, 128], I32), "cf": ("sbuf", [128, 64], F32), "cs": ("sbuf", [128, 160], BF),
+    "cu": ("sbuf", [128, 64], U16),
+    "wide": ("sbuf", [128, 5 * C], BF), "jc": ("sbuf", [128, C], BF), "iall": ("sbuf", [128, C + 8], F32),
+    "ef": ("sbuf", [128, C], F32), "yt": ("sbuf", [128, C], F32),
+}
+for _r in range(R + 1):
+    SCRATCH["x%d" % _r] = ("sbuf", [128, 4 * C], BF)
+    SCRATCH["qx%d" % _r] = ("sbuf", [128, C], X4)
+    SCRATCH["sx%d" % _r] = ("sbuf", [128, C], U8)
+for _r in range(R):
+    for _n, _w, _d in (("lq", C, X4), ("ls", C, U8), ("li", NW, U16), ("le", NW, U16),
+                       ("dt", 4 * C, BF), ("z", 4 * C, BF), ("zs", 4 * C, BF), ("xs", 4 * C, BF),
+                       ("qz", C, X4), ("sz", C, U8),
+                       ("pm", C, F32), ("pw", C, F32), ("eq", C, BF), ("ne", C, BF),
+                       ("fl", NV * C, BF), ("sb", NW * H, BF), ("sg", (NW - NV) * C, BF), ("acc", 64, F32),
+                       ("oc_", C, BF), ("ec", C, BF), ("tab", 8 * C, BF), ("hs", 10 * C, BF),
+                       ("ka", 10 * C, F32), ("kb", 9 * C, F32), ("tl", 3 * C, F32), ("pc", C, BF),
+                       ("off", 12 * NW, U16), ("oe", 4 * NW, U16)):
+        SCRATCH["%s%d" % (_n, _r)] = ("sbuf", [128, _w], _d)
+
+POOLS = {"v": 44, "s": 36, "t": 12, "g": 10, "d": 24}
+SEMAPHORES = ["%s%d" % (k, i) for k in POOLS for i in range(POOLS[k])] + ["sent"] + \
+    ["%s%d" % (k, r) for k in ("aq", "ai", "ae") for r in range(R)]
+
+
+def make_plan():
+    return {"ops": [], "groups": {}}
+
+
+def add(plan, queue, fn, deps=(), group=None, dma=False):
+    ops = plan["ops"]
+    ops.append({"q": queue, "fn": fn, "deps": [d for d in deps if d is not None], "group": group, "dma": dma})
+    i = len(ops) - 1
+    if group is not None:
+        plan["groups"].setdefault(group, []).append(i)
+        return group
+    return i
+
+
+def emit(plan, queues, sem):
+    ops, groups = plan["ops"], plan["groups"]
+    known = {q: set() for q in queues}
+    past, waits, needed = {}, [], set()
+    for i, op in enumerate(ops):
+        mine, w = known[op["q"]], []
+        for d in op["deps"]:
+            if d in mine:
+                continue
+            w.append(d)
+            needed.add(d)
+            mine.add(d)
+            for m in (groups[d] if d in groups else [d]):
+                mine |= past.get(m, set())
+        waits.append(w)
+        past[i] = set(mine)
+    last, count, where = {}, {}, {}
+    for i, op in enumerate(ops):
+        q = queues[op["q"]]
+        for d in waits[i]:
+            if isinstance(d, tuple):
+                q.wait_ge(sem[d[0]], d[1])
+            else:
+                q.wait_ge(sem[where[d]], where[d, "n"])
+        if op["fn"] is None:
+            continue
+        ins = op["fn"]()
+        key = op["group"] if op["group"] is not None else i
+        if key not in needed:
+            continue
+        step = 16 if op["dma"] else 1
+        if key not in where:
+            pool = "d" if op["dma"] else op["q"]
+            free = [n for n in ("%s%d" % (pool, k) for k in range(POOLS[pool])) if n not in last or last[n] in past[i]]
+            name = free[0]
+            last[name] = key
+            where[key] = name
+            count[name] = count.get(name, 0) + step * len(groups.get(key, [i]))
+            where[key, "n"] = count[name]
+        ins.then_inc(sem[where[key]], step)
+
+
+def rank_program(g, core, T, topo):
+    rank = T.rank_of(core)
+    if rank is None:
+        return
+    plan = make_plan()
+    V, A, PE = g.vector, g.scalar, g.tensor
+
+    def v(fn, deps=(), group=None):
+        return add(plan, "v", fn, deps, group)
+
+    def s(fn, deps=(), group=None):
+        return add(plan, "s", fn, deps, group)
+
+    def pe(fn, deps=(), group=None):
+        return add(plan, "t", fn, deps, group)
+
+    def gp(fn, deps=(), group=None):
+        return add(plan, "g", fn, deps, group)
+
+    def dma(queue, out, in_, deps=(), group=None):
+        eng = g.sync if queue == "y" else g.scalar
+        return add(plan, queue, lambda: eng.dma_start(out, in_), deps, group, dma=True)
+
+    def ts(out, in0, s1, op0, s2=None, op1=None, deps=(), group=None):
+        if op1 is None:
+            return v(lambda: V.tensor_scalar(out, in0, s1, None, op0), deps, group)
+        return v(lambda: V.tensor_scalar(out, in0, s1, s2, op0, op1), deps, group)
+
+    def tt(out, in0, in1, op, deps=(), group=None):
+        return v(lambda: V.tensor_tensor(out, in0, in1, op), deps, group)
+
+    def scan(out, d0, d1, init, op0, op1, deps=(), group=None):
+        return v(lambda: V.tensor_tensor_scan(out, d0, d1, init, op0, op1), deps, group)
+
+    def cp(out, in_, deps=(), group=None):
+        return v(lambda: V.tensor_copy(out, in_), deps, group)
+
+    def act(out, in_, func, deps=(), group=None, **kw):
+        return s(lambda: A.activation(out, in_, func, **kw), deps, group)
+
+    def quant(q, sc, in_, deps=(), group=None):
+        return v(lambda: V.quantize_mx(q, sc, in_), deps, group)
+
+    def mm(bank, n, lq, ls, rq, rs, deps=(), group=None):
+        return pe(lambda: PE.matmul_mx(T.ps[:, 512 * bank:512 * bank + n], lq, ls, rq, rs, True, True), deps, group)
+
+    def bank(b, lo, hi):
+        return T.ps[:, 512 * b + lo:512 * b + hi]
+
+    sends = [0]
+
+    def remote(dst, out, in_, name, deps):
+        rid, pid, ring = topo.addr(dst)
+        sends[0] += len(topo.engines(core, dst))
+        return gp(lambda: g.remote_dma(out, in_, T.sem[name], T.sem.sent, pid, rid, topo.mask(core, dst)), deps)
+
+    ld_u = dma("s", T.ut[:], T.u[:])
+    ld_x = [dma("y", T.x0[:, 0:2 * C], T.x[:, 0:2 * C]), dma("y", T.x0[:, 2 * C:4 * C], T.x[:, 2 * C:4 * C])]
+    ld_w = dma("y", T.qw[:].bitcast(dt.uint8), T.wc[:], group="ldw")
+    dma("y", T.sw[:], T.ws[:], group="ldw")
+    ld_v = dma("y", T.vt[:], T.v[:])
+
+    fl_ok = {"allow_small_or_imprecise_dtypes": True}
+    ip = gp(lambda: g.iota(T.ci[:, 0:NW], [[0, NW]], 0, 1))
+    iu = gp(lambda: g.iota(T.ci[:, 96:104], [[16, 8]], 0, 0))
+    it = gp(lambda: g.iota(T.cf[:, 0:16], [[1, 16]], 0, 0, **fl_ok))
+    one = v(lambda: V.memset(T.ones[:], 1.0))
+    c_e = gp(lambda: g.affine_select(T.et[:], T.ones[:], [[-1, 528]], ALU.is_equal, 0.0, 3, 4), [one])
+    c_jc = gp(lambda: g.iota(T.jc[:], [[1, C]], -H, 0, **fl_ok))
+    c_i = gp(lambda: g.iota(T.iall[:], [[512, C + 8]], -H - 512, 0, **fl_ok))
+    key_i, key_prev = T.iall[:, 1:C + 1], T.iall[:, 0:C]
+
+    qi = ts(T.ci[:, 24:48], T.ci[:, 0:NW], 15, ALU.bitwise_and, deps=[ip])
+    ri = ts(T.ci[:, 48:72], T.ci[:, 0:NW], 3, ALU.bitwise_and, deps=[ip])
+    hi = ts(T.ci[:, 72:74], T.ci[:, 0:2], 2, ALU.logical_shift_right, 3, ALU.bitwise_and, deps=[ip])
+    uo = cp(T.cu[:, 48:56], T.ci[:, 96:104], [iu])
+    qo = cp(T.cu[:, 0:24], T.ci[:, 24:48], [qi])
+    qf = cp(T.cf[:, 16:17], T.ci[:, 24:25], [qi])
+    ro = cp(T.cu[:, 24:48], T.ci[:, 48:72], [ri])
+    rf = cp(T.cf[:, 17:18], T.ci[:, 48:49], [ri])
+    hf = cp(T.cf[:, 18:19], T.ci[:, 72:73], [hi])
+    t16, qcol, rcol, hcol = T.cf[:, 0:16], T.cf[:, 16:17], T.cf[:, 17:18], T.cf[:, 18:19]
+
+    def small(k):
+        return T.cs[:, 16 * k:16 * k + 16]
+
+    k_mask = ts(small(0), t16, qcol, ALU.is_equal, deps=[it, qf])
+    k_reset = ts(small(1), t16, 0.0, ALU.is_gt, deps=[it])
+    k_a16 = ts(small(2), t16, qcol, ALU.is_gt, deps=[it, qf])
+    k_a4 = ts(small(5), t16, hcol, ALU.is_gt, deps=[it, hf])
+    k_b16 = ts(small(6), t16, qcol, ALU.subtract, 1.0, ALU.is_equal, deps=[it, qf])
+    k_b4 = ts(small(7), t16, hcol, ALU.subtract, 1.0, ALU.is_equal, deps=[it, hf])
+    k_sc = ts(T.cf[:, 20:21], qcol, 15.0, ALU.is_equal, 1.0 / BIG, ALU.max, deps=[qf])
+    k_s4 = ts(T.cf[:, 23:24], hcol, 3.0, ALU.is_equal, 1.0 / BIG, ALU.max, deps=[hf])
+    k_c16 = ts(small(8), small(6), BIG, ALU.mult, deps=[k_b16])
+    k_c4 = ts(small(9), small(7), BIG, ALU.mult, deps=[k_b4])
+    k_scm = ts(T.cf[:, 21:22], T.cf[:, 20:21], 1.0 / 512, ALU.mult, deps=[k_sc])
+    k_sc4 = ts(T.cf[:, 22:23], T.cf[:, 23:24], 4.0, ALU.mult, deps=[k_s4])
+    k_add4 = ts(T.cf[:, 24:25], rcol, 4.0 * H, ALU.add, deps=[rf])
+    k_h16 = tt(small(3), small(8), small(2), ALU.max, [k_c16, k_a16])
+    k_h4 = tt(small(4), small(9), small(5), ALU.max, [k_c4, k_a4])
+    sc16, scm, sc4, add4 = T.cf[:, 20:21], T.cf[:, 21:22], T.cf[:, 22:23], T.cf[:, 24:25]
+
+    def wide(k):
+        return T.wide[:, C * k:C * k + C]
+
+    w_mask = act(wide(0), small(0).indirect(T.cu[:, 0:24]), ACT.Copy, [k_mask, qo])
+    w_reset = act(wide(1), small(1).indirect(T.cu[:, 0:24]), ACT.Copy, [k_reset, qo])
+    w_a16 = act(wide(2), small(2).indirect(T.cu[:, 0:24]), ACT.Copy, [k_a16, qo])
+    w_h16 = act(wide(3), small(3).indirect(T.cu[:, 0:24]), ACT.Copy, [k_h16, qo])
+    w_h4 = act(wide(4), small(4).indirect(T.cu[:, 24:48]), ACT.Copy, [k_h4, ro])
+
+    q_u = quant(T.qu[:], T.su[:], T.ut[:], [ld_u])
+    cp(T.qur[:].bitcast(dt.uint32), T.qu[:].bitcast(dt.uint32).indirect(T.cu[:, 48:56]), [q_u, uo], group="ur")
+    q_ur = cp(T.sur[:], T.su[:].indirect(T.cu[:, 48:56]), [q_u, uo], group="ur")
+    for r in range(R):
+        fill = v(lambda r=r: V.memset(T["oc_%d" % r][:], 0.0), group="fill")
+        v(lambda r=r: V.memset(T["ec%d" % r][:], 0.0), group="fill")
+    for b in range(4):
+        q_e = quant(T.qe[:, 128 * b:128 * b + 128], T.se[:, 128 * b:128 * b + 128], T.et[:, 3 - b:3 - b + 512], [c_e], group="qe")
+    q_x = [quant(T.qx0[:, 0:H], T.sx0[:, 0:H], T.x0[:, 0:2 * C], [ld_x[0]]),
+           quant(T.qx0[:, H:C], T.sx0[:, H:C], T.x0[:, 2 * C:4 * C], [ld_x[1]])]
+    x_made = list(ld_x)
+    psum_free = []
+    q_v = None
+
+    for r in range(R):
+        mate = T.cores[rank ^ STEP[r]]
+        ne = len(topo.engines(mate, core))
+
+        def B(name, r=r):
+            return T["%s%d" % (name, r)]
+
+        X, qx, sx = B("x"), B("qx"), B("sx")
+        off = B("off")
+
+        def offs(k):
+            return off[:, NW * k:NW * k + NW]
+
+        def part(buf, k):
+            return buf[:, C * k:C * k + C]
+
+        p_v = mm(0, C, T.qur[:], T.sur[:], qx[:], sx[:], q_x + [q_ur] + psum_free)
+        p_s = mm(1, C, T.qur[:], T.sur[:], qx[:], sx[:], q_x + [q_ur] + psum_free)
+        remote(mate, B("lq")[:].bitcast(dt.uint8), qx[:].bitcast(dt.uint8), "aq%d" % r, q_x)
+        remote(mate, B("ls")[:], sx[:], "aq%d" % r, q_x)
+        d_mm = [mm(2 + b, C, T.qe[:, 128 * b:128 * b + 128], T.se[:, 128 * b:128 * b + 128], B("lq")[:], B("ls")[:],
+                   [q_e, ("aq%d" % r, 2 * ne)] + psum_free) for b in range(4)]
+
+        pm = tt(B("pm")[:], bank(0, 0, C), wide(0), ALU.mult, [p_v, w_mask])
+        pw = scan(B("pw")[:], wide(1), B("pm")[:], 0.0, ALU.mult, ALU.add, [pm, w_reset])
+        eq = tt(B("eq")[:], B("pw")[:], bank(0, 0, C), ALU.is_equal, [pw])
+        fl, sb, sg, acc = B("fl"), B("sb"), B("sg"), B("acc")
+        for c in range(NV, NW):
+            k, cut = c - NV, 16 * c + 16
+            row = sg[:, C * k:C * k + C]
+            s1 = act(row, bank(1, 0, C), ACT.Sign, [p_s, pw], bias=B("pw")[:, 16 * c + 15:16 * c + 16], scale=-1.0)
+            if k > 0:
+                pend()
+            def pend(k=k, cut=cut, s1=s1):
+                act(sg[:, C * k:C * k + cut], sg[:, C * k:C * k + cut], ACT.Sign, [s1], group="acc%d" % r,
+                    bias=0.5, scale=-1.0, accum_out=acc[:, k:k + 1])
+                if cut < C:
+                    act(sg[:, C * k + cut:C * k + C], sg[:, C * k + cut:C * k + C], ACT.Sign, [s1], group="acc%d" % r,
+                        bias=-0.5, scale=-1.0, accum_out=acc[:, 16 + k:17 + k])
+        pend()
+        nz = v(lambda acc=acc: V.memset(acc[:, 16 + NW - NV - 1:16 + NW - NV], 0.0))
+        cmps = []
+        neq = None
+        for c in range(NV):
+            cut = 16 * c + 16
+            col = B("pw")[:, 16 * c + 15:16 * c + 16]
+            gname = "cmp%d_%d" % (r, c)
+            ts(fl[:, C * c:C * c + cut], bank(0, 0, cut), col, ALU.is_ge, 0.5, ALU.subtract, [pw], group=gname)
+            ts(fl[:, C * c + cut:C * c + C], bank(0, cut, C), col, ALU.is_gt, 0.5, ALU.subtract, [pw], group=gname)
+            cmps.append(gname)
+            if c == 0:
+                neq = scan(B("ne")[:], wide(2), B("eq")[:], 0.0, ALU.mult, ALU.subtract, [eq, w_a16])
+            else:
+                d = c - 1
+                scan(sb[:, H * d:H * d + H], fl[:, C * d:C * d + H], fl[:, C * d + H:C * d + C],
+                     B("ne")[:, 16 * d + 15:16 * d + 16], ALU.add, ALU.add, [cmps[d], neq], group="cnt%d" % r)
+        n = NW - NV
+        a1 = tt(acc[:, 32:32 + n], acc[:, 0:n], acc[:, 16:16 + n], ALU.add, ["acc%d" % r, nz])
+        d = NV - 1
+        scan(sb[:, H * d:H * d + H], fl[:, C * d:C * d + H], fl[:, C * d + H:C * d + C],
+             B("ne")[:, 16 * d + 15:16 * d + 16], ALU.add, ALU.add, [cmps[d], neq], group="cnt%d" % r)
+        a2 = ts(acc[:, 48:48 + n], acc[:, 32:32 + n], 0.5, ALU.mult, deps=[a1])
+        cnt = tt(sb[:, H * NV + H - 1:H * NW:H], acc[:, 48:48 + n], B("ne")[:, 16 * NV + 15:C:16], ALU.add, [a2, neq], group="cnt%d" % r)
+        i_w = ts(offs(0), sb[:, H - 1:H * NW:H], float(H), ALU.add, deps=[cnt])
+        remote(mate, B("li")[:], offs(0), "ai%d" % r, [i_w])
+        o_c = cp(B("oc_")[:].indirect(offs(0)), T.jc[:], [i_w, c_jc, fill])
+        if q_v is None:
+            q_v = quant(T.qv[:], T.sv[:], T.vt[:], [ld_v])
+        for b in range(4):
+            d_cp = act(B("dt")[:, b:4 * C:4], bank(2 + b, 0, C), ACT.Copy, [d_mm[b]], group="dcp%d" % r)
+
+        tab, hs, ka, kb = B("tab"), B("hs"), B("ka"), B("kb")
+        came = ("ai%d" % r, ne)
+
+        def wrap(src, k, dst, deps):
+            h = scan(part(hs, k), wide(3), src, 0.0, ALU.mult, ALU.add, deps + [w_h16])
+            return ts(dst, hs[:, C * k + 15:C * k + C:16], sc16, ALU.mult, float(H), ALU.add, [h, k_sc])
+
+        t_k = act(part(tab, 0), B("oc_")[:].indirect(B("li")[:]), ACT.Copy, [o_c, came])
+        a_k = ts(part(ka, 0), B("oc_")[:].indirect(B("li")[:]), 512.0, ALU.mult, 512.0 * H + H, ALU.add, [o_c, came])
+        b_k = act(part(kb, 0), part(ka, 0), ACT.Identity, [a_k], bias=-1.0)
+        o_k = wrap(part(tab, 0), 0, offs(1), [t_k])
+        for k in range(8):
+            if k < 7:
+                t_n = act(part(tab, k + 1), part(tab, k).indirect(offs(k + 1)), ACT.Copy, [t_k, o_k])
+            else:
+                b_last = act(part(kb, 8), part(ka, 7), ACT.Identity, [a_k], bias=-256.0)
+            a_n = tt(part(ka, k + 1), part(ka, k).indirect(offs(k + 1)), part(kb, k), ALU.min, [a_k, b_k, o_k])
+            if k < 7:
+                b_k = act(part(kb, k + 1), part(ka, k + 1), ACT.Identity, [a_n], bias=-float(2 ** (k + 1)))
+                o_k = wrap(part(tab, k + 1), k + 1, offs(k + 2), [t_n])
+                t_k = t_n
+            a_k = a_n
+        key = part(ka, 9)
+        a_k = tt(key, part(ka, 8).indirect(offs(8)), part(kb, 8), ALU.min, [a_k, b_last, o_k])
+        tl = B("tl")
+        h_m = scan(part(tl, 0), wide(3), key, 0.0, ALU.mult, ALU.add, [a_k, w_h16])
+        top = scan(part(tl, 1), key, key_i, -1.0e6, ALU.max, ALU.max, [a_k, c_i])
+        m1 = ts(acc[:, 0:NW], tl[:, 15:C:16], scm, ALU.mult, MAGIC, ALU.add, [h_m, k_scm, a1])
+        ends = scan(part(tl, 2), part(tl, 1), key_prev, -512.0 - 2 * H, ALU.add, ALU.subtract, [top])
+        m2 = ts(offs(9), acc[:, 0:NW], MAGIC, ALU.subtract, deps=[m1])
+        pos = tt(B("pc")[:], part(tl, 2).indirect(offs(9)), key, ALU.subtract, [ends, m2])
+        o_p = wrap(B("pc")[:], 8, offs(10), [pos])
+        e_c = cp(B("ec")[:].indirect(offs(10)), T.jc[:], [o_p, fill])
+        h_e = scan(part(hs, 9), wide(4), B("ec")[:], 0.0, ALU.mult, ALU.add, [e_c, w_h4])
+        oe = B("oe")
+        o_e = ts(oe[:], hs[:, 9 * C + 3:10 * C:4], sc4, ALU.mult, add4, ALU.add, [h_e, k_sc4, k_add4])
+        remote(mate, B("le")[:], oe[:, 0:NW], "ae%d" % r, [o_e])
+
+        Z, zs, xs, qz, sz = B("z"), B("zs"), B("xs"), B("qz"), B("sz")
+        Xn, qn, sn = T["x%d" % (r + 1)], T["qx%d" % (r + 1)], T["sx%d" % (r + 1)]
+        ga1 = cp(Z[:, 512:1024], X[:].indirect(oe[:, 32:64]), [o_e] + x_made)
+        ga2 = act(Z[:, 1024:1536], X[:].indirect(oe[:, 64:96]), ACT.Copy, [o_e] + x_made)
+        q_a = quant(qz[:, 128:C], sz[:, 128:C], Z[:, 512:1536], [ga1, ga2])
+        za2 = act(zs[:, 1024:1536], Z[:, 1024:1536], ACT.Copy, [ga2], scale=64.0)
+        za1 = ts(zs[:, 512:1024], Z[:, 512:1024], 64.0, ALU.mult, deps=[ga1])
+        gb1 = act(Z[:, 384:512], X[:].indirect(oe[:, 24:32]), ACT.Copy, [o_e])
+        gb2 = act(Z[:, 0:384], B("dt")[:].indirect(B("le")[:]), ACT.Copy, [d_cp, ("ae%d" % r, ne)])
+        zb = act(zs[:, 0:512], Z[:, 0:512], ACT.Copy, [gb1, gb2], scale=64.0)
+        if r == R - 1:
+            e_f = act(T.ef[:], B("ec")[:], ACT.Identity, [e_c], bias=float(H))
+            st_e = dma("y", T.el[:], T.ef[0:128:16, :], [e_f], group="st")
+
+        def wb(b):
+            return T.qw[:, 128 * b:128 * b + 128], T.sw[:, 128 * b:128 * b + 128]
+
+        m_a = [mm(b, 256, wb(b)[0], wb(b)[1], qz[:, 128:C], sz[:, 128:C], [q_a, ld_w, d_cp, cnt]) for b in range(4)]
+        for b in range(4):
+            r_a = tt(xs[:, 512 + b:1536:4], bank(b, 0, 256), zs[:, 512 + b:1536:4], ALU.add, [m_a[b], za1, za2], group="ra%d" % r)
+        q_b = quant(qz[:, 0:128], sz[:, 0:128], Z[:, 0:512], [gb1, gb2])
+        m_b = [mm(4 + b, 128, wb(b)[0], wb(b)[1], qz[:, 0:128], sz[:, 0:128], [q_b]) for b in range(4)]
+        x_a = ts(Xn[:, 512:1536], xs[:, 512:1536], 0.015625, ALU.mult, deps=[r_a])
+        for b in range(4):
+            r_b = tt(xs[:, b:512:4], bank(4 + b, 0, 128), zs[:, b:512:4], ALU.add, [m_b[b], zb], group="rb%d" % r)
+        n_a = quant(qn[:, 128:C], sn[:, 128:C], Xn[:, 512:1536], [x_a])
+        x_b = ts(Xn[:, 0:512], xs[:, 0:512], 0.015625, ALU.mult, deps=[r_b])
+        n_b = quant(qn[:, 0:128], sn[:, 0:128], Xn[:, 0:512], [x_b])
+        q_x, x_made, psum_free = [n_a, n_b], [x_a, x_b], [r_a, r_b]
+
+    qn, sn = T["qx%d" % R], T["sx%d" % R]
+    y_a = mm(0, 256, T.qv[:], T.sv[:], qn[:, 128:C], sn[:, 128:C], [q_x[0], q_v, psum_free[0]])
+    y_b = mm(1, 128, T.qv[:], T.sv[:], qn[:, 0:128], sn[:, 0:128], [q_x[1]])
+    dma("y", T.oc[:, 512:1536], qn[:, 128:C].bitcast(dt.uint8), [q_x[0]], group="st")
+    c_a = act(T.yt[:, 128:C], bank(0, 0, 256), ACT.Copy, [y_a])
+    dma("s", T.y[:, 128:C], T.yt[:, 128:C], [c_a], group="st")
+    c_b = cp(T.yt[:, 0:128], bank(1, 0, 128), [y_b])
+    dma("y", T.oc[:, 0:512], qn[:, 0:128].bitcast(dt.uint8), [q_x[1]], group="st")
+    for k in range(4):
+        dma("ys"[k % 2], T.osc[4 * k:4 * k + 4, :], sn[32 * k:32 * k + 4, :], q_x, group="st")
+    dma("y", T.y[:, 0:128], T.yt[:, 0:128], [c_b], group="st")
+    add(plan, "y", None, ["st"])
+    add(plan, "g", None, [("sent", sends[0])])
+    emit(plan, {"v": V, "s": A, "t": PE, "g": g, "y": g.sync}, T.sem)

@@ -5,11 +5,17 @@ ACT = ActivationFunctionType
 C, S, R = 384, 96, 2
 STEP = [2, 1]
 NW = C // 16
-NV = 15
+S0, S1 = 13, 21
+NT = NW // 4
 BIG = 2.0 ** 40
-MAGIC = 12582912.0
+FAR = 2.0 ** 96
+KEY = 1024.0
 H = C // 2
 X4, U8, BF, F32, U16, I32 = "float8_e4m3fn_x4", "uint8", "bfloat16", "float32", "uint16", "int32"
+WIDTH = [64 * a + 64 for a in range(NT)]
+START = [sum(WIDTH[a + 1:]) for a in range(NT)]
+WORDS = sum(WIDTH) + 64
+SCALAR_TILES = [4, 3, 0]
 
 SCRATCH = {
     "ps": ("psum", [128, 4096], F32),
@@ -20,9 +26,13 @@ SCRATCH = {
     "qw": ("sbuf", [128, 512], X4), "sw": ("sbuf", [128, 512], U8),
     "ones": ("sbuf", [128, 528], BF), "et": ("sbuf", [128, 528], BF),
     "qe": ("sbuf", [128, 512], X4), "se": ("sbuf", [128, 512], U8),
-    "ci": ("sbuf", [128, 128], I32), "cf": ("sbuf", [128, 64], F32), "cs": ("sbuf", [128, 160], BF),
-    "cu": ("sbuf", [128, 64], U16),
-    "wide": ("sbuf", [128, 5 * C], BF), "jc": ("sbuf", [128, C], BF), "iall": ("sbuf", [128, C + 8], F32),
+    "bw": ("sbuf", [128, 1024], BF), "qb": ("sbuf", [128, 256], X4), "sq": ("sbuf", [128, 256], U8),
+    "ci": ("sbuf", [128, 64], I32), "cf": ("sbuf", [128, 64], F32), "cs": ("sbuf", [128, 160], BF),
+    "cu": ("sbuf", [128, 96], U16),
+    "wide": ("sbuf", [128, 4 * C], BF), "jr": ("sbuf", [128, C], BF), "jc": ("sbuf", [128, C], BF),
+    "iall": ("sbuf", [128, C + 8], F32),
+    "ft": ("sbuf", [128, 4 * WORDS], BF), "qf": ("sbuf", [128, WORDS], X4), "sf": ("sbuf", [128, WORDS], U8),
+    "sg": ("sbuf", [128, S1 * C], BF), "sb": ("sbuf", [128, NW * H], BF),
     "ef": ("sbuf", [128, C], F32), "yt": ("sbuf", [128, C], F32),
 }
 for _r in range(R + 1):
@@ -33,14 +43,13 @@ for _r in range(R):
     for _n, _w, _d in (("lq", C, X4), ("ls", C, U8), ("li", NW, U16), ("le", NW, U16),
                        ("dt", 4 * C, BF), ("z", 4 * C, BF), ("zs", 4 * C, BF), ("xs", 4 * C, BF),
                        ("qz", C, X4), ("sz", C, U8),
-                       ("pm", C, F32), ("pw", C, F32), ("eq", C, BF), ("ne", C, BF),
-                       ("fl", NV * C, BF), ("sb", NW * H, BF), ("sg", (NW - NV) * C, BF), ("acc", 64, F32),
+                       ("pm", C, F32), ("pw", C, F32), ("ne", C, BF), ("hc", C, BF), ("acc", 96, F32),
                        ("oc_", C, BF), ("ec", C, BF), ("tab", 8 * C, BF), ("hs", 10 * C, BF),
                        ("ka", 10 * C, F32), ("kb", 9 * C, F32), ("tl", 3 * C, F32), ("pc", C, BF),
                        ("off", 12 * NW, U16), ("oe", 4 * NW, U16)):
         SCRATCH["%s%d" % (_n, _r)] = ("sbuf", [128, _w], _d)
 
-POOLS = {"v": 44, "s": 36, "t": 12, "g": 10, "d": 24}
+POOLS = {"v": 48, "s": 36, "t": 12, "g": 10, "d": 24}
 SEMAPHORES = ["%s%d" % (k, i) for k in POOLS for i in range(POOLS[k])] + ["sent"] + \
     ["%s%d" % (k, r) for k in ("aq", "ai", "ae") for r in range(R)]
 
@@ -65,7 +74,7 @@ def emit(plan, queues, sem):
     past, waits, needed = {}, [], set()
     for i, op in enumerate(ops):
         mine, w = known[op["q"]], []
-        for d in op["deps"]:
+        for d in reversed(op["deps"]):
             if d in mine:
                 continue
             w.append(d)
@@ -144,8 +153,8 @@ def rank_program(g, core, T, topo):
     def quant(q, sc, in_, deps=(), group=None):
         return v(lambda: V.quantize_mx(q, sc, in_), deps, group)
 
-    def mm(bank, n, lq, ls, rq, rs, deps=(), group=None):
-        return pe(lambda: PE.matmul_mx(T.ps[:, 512 * bank:512 * bank + n], lq, ls, rq, rs, True, True), deps, group)
+    def mm(bank, n, lq, ls, rq, rs, deps=(), group=None, start=True, stop=True):
+        return pe(lambda: PE.matmul_mx(T.ps[:, 512 * bank:512 * bank + n], lq, ls, rq, rs, start, stop), deps, group)
 
     def bank(b, lo, hi):
         return T.ps[:, 512 * b + lo:512 * b + hi]
@@ -159,73 +168,86 @@ def rank_program(g, core, T, topo):
 
     ld_u = dma("s", T.ut[:], T.u[:])
     ld_x = [dma("y", T.x0[:, 0:2 * C], T.x[:, 0:2 * C]), dma("y", T.x0[:, 2 * C:4 * C], T.x[:, 2 * C:4 * C])]
-    ld_w = dma("y", T.qw[:].bitcast(dt.uint8), T.wc[:], group="ldw")
+    ld_w = dma("y", T.qw[:].bitcast(dt.uint8), T.wc[:], ld_x, group="ldw")
     dma("y", T.sw[:], T.ws[:], group="ldw")
     ld_v = dma("y", T.vt[:], T.v[:])
 
     fl_ok = {"allow_small_or_imprecise_dtypes": True}
-    ip = gp(lambda: g.iota(T.ci[:, 0:NW], [[0, NW]], 0, 1))
-    iu = gp(lambda: g.iota(T.ci[:, 96:104], [[16, 8]], 0, 0))
-    it = gp(lambda: g.iota(T.cf[:, 0:16], [[1, 16]], 0, 0, **fl_ok))
-    one = v(lambda: V.memset(T.ones[:], 1.0))
-    c_e = gp(lambda: g.affine_select(T.et[:], T.ones[:], [[-1, 528]], ALU.is_equal, 0.0, 3, 4), [one])
-    c_jc = gp(lambda: g.iota(T.jc[:], [[1, C]], -H, 0, **fl_ok))
-    c_i = gp(lambda: g.iota(T.iall[:], [[512, C + 8]], -H - 512, 0, **fl_ok))
-    key_i, key_prev = T.iall[:, 1:C + 1], T.iall[:, 0:C]
+    ip = gp(lambda: g.iota(T.ci[:, 0:2], [[0, 2]], 0, 1))
+    gp(lambda: g.iota(T.ci[:, 16:24], [[16, 8]], 0, 0), group="iu")
+    iu = gp(lambda: g.iota(T.ci[:, 24:56], [[1, 8], [0, 4]], 0, 0), group="iu")
+    it = gp(lambda: g.iota(T.cf[:, 0:NW + 1], [[1, NW + 1]], -1, 0, **fl_ok))
+    c_jr = gp(lambda: g.iota(T.jr[:], [[0, NW], [1, 16]], 0, 0, **fl_ok))
+    one = gp(lambda: g.iota(T.ones[:], [[0, 528]], 1, 0, **fl_ok))
 
-    qi = ts(T.ci[:, 24:48], T.ci[:, 0:NW], 15, ALU.bitwise_and, deps=[ip])
-    ri = ts(T.ci[:, 48:72], T.ci[:, 0:NW], 3, ALU.bitwise_and, deps=[ip])
-    hi = ts(T.ci[:, 72:74], T.ci[:, 0:2], 2, ALU.logical_shift_right, 3, ALU.bitwise_and, deps=[ip])
-    uo = cp(T.cu[:, 48:56], T.ci[:, 96:104], [iu])
-    qo = cp(T.cu[:, 0:24], T.ci[:, 24:48], [qi])
-    qf = cp(T.cf[:, 16:17], T.ci[:, 24:25], [qi])
-    ro = cp(T.cu[:, 24:48], T.ci[:, 48:72], [ri])
-    rf = cp(T.cf[:, 17:18], T.ci[:, 48:49], [ri])
-    hf = cp(T.cf[:, 18:19], T.ci[:, 72:73], [hi])
-    t16, qcol, rcol, hcol = T.cf[:, 0:16], T.cf[:, 16:17], T.cf[:, 17:18], T.cf[:, 18:19]
+    def col(k):
+        return T.cf[:, k:k + 1]
 
     def small(k):
         return T.cs[:, 16 * k:16 * k + 16]
 
-    k_mask = ts(small(0), t16, qcol, ALU.is_equal, deps=[it, qf])
-    k_reset = ts(small(1), t16, 0.0, ALU.is_gt, deps=[it])
-    k_a16 = ts(small(2), t16, qcol, ALU.is_gt, deps=[it, qf])
-    k_a4 = ts(small(5), t16, hcol, ALU.is_gt, deps=[it, hf])
-    k_b16 = ts(small(6), t16, qcol, ALU.subtract, 1.0, ALU.is_equal, deps=[it, qf])
-    k_b4 = ts(small(7), t16, hcol, ALU.subtract, 1.0, ALU.is_equal, deps=[it, hf])
-    k_sc = ts(T.cf[:, 20:21], qcol, 15.0, ALU.is_equal, 1.0 / BIG, ALU.max, deps=[qf])
-    k_s4 = ts(T.cf[:, 23:24], hcol, 3.0, ALU.is_equal, 1.0 / BIG, ALU.max, deps=[hf])
-    k_c16 = ts(small(8), small(6), BIG, ALU.mult, deps=[k_b16])
-    k_c4 = ts(small(9), small(7), BIG, ALU.mult, deps=[k_b4])
-    k_scm = ts(T.cf[:, 21:22], T.cf[:, 20:21], 1.0 / 512, ALU.mult, deps=[k_sc])
-    k_sc4 = ts(T.cf[:, 22:23], T.cf[:, 23:24], 4.0, ALU.mult, deps=[k_s4])
-    k_add4 = ts(T.cf[:, 24:25], rcol, 4.0 * H, ALU.add, deps=[rf])
-    k_h16 = tt(small(3), small(8), small(2), ALU.max, [k_c16, k_a16])
-    k_h4 = tt(small(4), small(9), small(5), ALU.max, [k_c4, k_a4])
-    sc16, scm, sc4, add4 = T.cf[:, 20:21], T.cf[:, 21:22], T.cf[:, 22:23], T.cf[:, 24:25]
-
     def wide(k):
         return T.wide[:, C * k:C * k + C]
 
-    w_mask = act(wide(0), small(0).indirect(T.cu[:, 0:24]), ACT.Copy, [k_mask, qo])
-    w_reset = act(wide(1), small(1).indirect(T.cu[:, 0:24]), ACT.Copy, [k_reset, qo])
-    w_a16 = act(wide(2), small(2).indirect(T.cu[:, 0:24]), ACT.Copy, [k_a16, qo])
-    w_h16 = act(wide(3), small(3).indirect(T.cu[:, 0:24]), ACT.Copy, [k_h16, qo])
-    w_h4 = act(wide(4), small(4).indirect(T.cu[:, 24:48]), ACT.Copy, [k_h4, ro])
+    def clear(a):
+        end = START[a] + WIDTH[a]
+        return v(lambda: V.memset(T.ft[:, 4 * (end - 48):4 * (end if a else WORDS)], 0.0), group="zero")
 
+    less1, t16, t24 = T.cf[:, 0:16], T.cf[:, 1:17], T.cf[:, 1:NW + 1]
+    qcol, gcol, rcol, hcol = col(32), col(33), col(34), col(35)
+    sc16, scm, sc4, add4, big16, base = col(36), col(37), col(38), col(39), col(40), col(41)
+    clear(0)
+    ts(T.ci[:, 4:5], T.ci[:, 0:1], 15, ALU.bitwise_and, deps=[ip], group="pi")
+    pi = ts(T.ci[:, 5:6], T.ci[:, 0:1], 4, ALU.logical_shift_right, deps=[ip], group="pi")
+    clear(1)
+    pf = cp(T.cf[:, 32:34], T.ci[:, 4:6], [pi])
+    uo = cp(T.cu[:, 48:88], T.ci[:, 16:56], [iu])
+    k_grp = ts(small(0), t16, gcol, ALU.is_equal, deps=[it, pf])
+    for a in range(2, NT):
+        zero = clear(a)
     q_u = quant(T.qu[:], T.su[:], T.ut[:], [ld_u])
-    cp(T.qur[:].bitcast(dt.uint32), T.qu[:].bitcast(dt.uint32).indirect(T.cu[:, 48:56]), [q_u, uo], group="ur")
-    q_ur = cp(T.sur[:], T.su[:].indirect(T.cu[:, 48:56]), [q_u, uo], group="ur")
-    for r in range(R):
-        fill = v(lambda r=r: V.memset(T["oc_%d" % r][:], 0.0), group="fill")
-        v(lambda r=r: V.memset(T["ec%d" % r][:], 0.0), group="fill")
-    for b in range(4):
-        q_e = quant(T.qe[:, 128 * b:128 * b + 128], T.se[:, 128 * b:128 * b + 128], T.et[:, 3 - b:3 - b + 512], [c_e], group="qe")
-    q_x = [quant(T.qx0[:, 0:H], T.sx0[:, 0:H], T.x0[:, 0:2 * C], [ld_x[0]]),
-           quant(T.qx0[:, H:C], T.sx0[:, H:C], T.x0[:, 2 * C:4 * C], [ld_x[1]])]
+    cp(T.qur[:].bitcast(dt.uint32), T.qu[:].bitcast(dt.uint32).indirect(T.cu[:, 48:56]), [uo, q_u], group="ur")
+    q_ur = cp(T.sur[:], T.su[:].indirect(T.cu[:, 48:56]), [uo, q_u], group="ur")
+    q_x = [quant(T.qx0[:, 0:H], T.sx0[:, 0:H], T.x0[:, 0:2 * C], [ld_x[0]])]
+    w_own = ts(wide(0), T.jr[:], qcol, ALU.not_equal, FAR, ALU.mult, [pf, c_jr])
+    q_x.append(quant(T.qx0[:, H:C], T.sx0[:, H:C], T.x0[:, 2 * C:4 * C], [ld_x[1]]))
+    w_new = ts(wide(1), T.jr[:], 0.0, ALU.is_equal, FAR, ALU.mult, [c_jr])
+    k_a16 = ts(small(2), t16, qcol, ALU.is_gt, deps=[it, pf])
+    k_c16 = ts(small(8), less1, qcol, ALU.is_equal, BIG, ALU.mult, [it, pf])
+    c_bd = act(T.bw[:, 0:512], small(0).indirect(T.cu[:, 56:88]), ACT.Copy, [uo, k_grp])
+    c_bw = act(T.bw[:, 512:1024], T.bw[:, 0:512], ACT.Copy, [c_bd], scale=0.5)
     x_made = list(ld_x)
     psum_free = []
-    q_v = None
+    late = {}
+    soon = [
+        lambda: late.update(h16=tt(small(3), small(8), small(2), ALU.max, [k_a16, k_c16])),
+        lambda: late.update(qo=ts(T.cu[:, 0:NW], t24, 0.0, ALU.mult, qcol, ALU.add, [it, pf])),
+        lambda: late.update(sc=ts(sc16, qcol, 15.0, ALU.is_equal, 1.0 / BIG, ALU.max, [pf])),
+        lambda: late.update(up=ts(col(42), qcol, 15.0, ALU.is_lt, BIG, ALU.mult, [pf])),
+        lambda: late.update(bd=quant(T.qb[:], T.sq[:], T.bw[:], [c_bw])),
+    ]
+
+    def unpacker(b):
+        return lambda: late.update(qe=quant(T.qe[:, 128 * b:128 * b + 128], T.se[:, 128 * b:128 * b + 128],
+                                            T.et[:, 3 - b:3 - b + 512], [late["et"]], group="qe"))
+
+    gaps = [
+        [lambda: ts(T.ci[:, 6:7], T.ci[:, 0:1], 3, ALU.bitwise_and, deps=[ip], group="pj"),
+         lambda: ts(T.ci[:, 7:8], T.ci[:, 0:1], 2, ALU.logical_shift_right, 3, ALU.bitwise_and, deps=[ip], group="pj")],
+        [lambda: late.update(pg=cp(T.cf[:, 34:36], T.ci[:, 6:8], ["pj"]))],
+        [lambda: late.update(a4=ts(small(5), t16, hcol, ALU.is_gt, deps=[it, late["pg"]])),
+         lambda: late.update(c4=ts(small(9), less1, hcol, ALU.is_equal, BIG, ALU.mult, [it, late["pg"]]))],
+        [lambda: late.update(ro=ts(T.cu[:, NW:2 * NW], t24, 0.0, ALU.mult, rcol, ALU.add, [it, late["pg"]])),
+         lambda: late.update(h4=tt(small(4), small(9), small(5), ALU.max, [late["a4"], late["c4"]]))],
+        [unpacker(0)], [unpacker(1)], [unpacker(2)], [unpacker(3)],
+        [lambda: late.update(s4=ts(col(43), hcol, 3.0, ALU.is_equal, 1.0 / BIG, ALU.max, [late["pg"]]))],
+        [lambda: late.update(qv=quant(T.qv[:], T.sv[:], T.vt[:], [ld_v]))],
+    ]
+
+    def gap():
+        if gaps:
+            for f in gaps.pop(0):
+                f()
 
     for r in range(R):
         mate = T.cores[rank ^ STEP[r]]
@@ -243,132 +265,183 @@ def rank_program(g, core, T, topo):
         def part(buf, k):
             return buf[:, C * k:C * k + C]
 
-        p_v = mm(0, C, T.qur[:], T.sur[:], qx[:], sx[:], q_x + [q_ur] + psum_free)
-        p_s = mm(1, C, T.qur[:], T.sur[:], qx[:], sx[:], q_x + [q_ur] + psum_free)
+        p_v = mm(0, C, T.qur[:], T.sur[:], qx[:], sx[:], [q_ur] + psum_free + q_x)
+        p_s = mm(1, C, T.qur[:], T.sur[:], qx[:], sx[:], [q_ur] + psum_free + q_x)
         remote(mate, B("lq")[:].bitcast(dt.uint8), qx[:].bitcast(dt.uint8), "aq%d" % r, q_x)
         remote(mate, B("ls")[:], sx[:], "aq%d" % r, q_x)
-        d_mm = [mm(2 + b, C, T.qe[:, 128 * b:128 * b + 128], T.se[:, 128 * b:128 * b + 128], B("lq")[:], B("ls")[:],
-                   [q_e, ("aq%d" % r, 2 * ne)] + psum_free) for b in range(4)]
+        if r == 0:
+            c_jc = gp(lambda: g.iota(T.jc[:], [[1, C]], -H, 0, **fl_ok))
+            late["et"] = gp(lambda: g.affine_select(T.et[:], T.ones[:], [[-1, 528]], ALU.is_equal, 0.0, 3, 4), [one])
+            c_i = gp(lambda: g.iota(T.iall[:], [[int(KEY), C + 8]], -int(KEY), 0, **fl_ok))
+        key_i, key_prev = T.iall[:, 1:C + 1], T.iall[:, 0:C]
 
-        pm = tt(B("pm")[:], bank(0, 0, C), wide(0), ALU.mult, [p_v, w_mask])
-        pw = scan(B("pw")[:], wide(1), B("pm")[:], 0.0, ALU.mult, ALU.add, [pm, w_reset])
-        eq = tt(B("eq")[:], B("pw")[:], bank(0, 0, C), ALU.is_equal, [pw])
-        fl, sb, sg, acc = B("fl"), B("sb"), B("sg"), B("acc")
-        for c in range(NV, NW):
-            k, cut = c - NV, 16 * c + 16
-            row = sg[:, C * k:C * k + C]
-            s1 = act(row, bank(1, 0, C), ACT.Sign, [p_s, pw], bias=B("pw")[:, 16 * c + 15:16 * c + 16], scale=-1.0)
-            if k > 0:
-                pend()
-            def pend(k=k, cut=cut, s1=s1):
-                act(sg[:, C * k:C * k + cut], sg[:, C * k:C * k + cut], ACT.Sign, [s1], group="acc%d" % r,
-                    bias=0.5, scale=-1.0, accum_out=acc[:, k:k + 1])
-                if cut < C:
-                    act(sg[:, C * k + cut:C * k + C], sg[:, C * k + cut:C * k + C], ACT.Sign, [s1], group="acc%d" % r,
-                        bias=-0.5, scale=-1.0, accum_out=acc[:, 16 + k:17 + k])
-        pend()
-        nz = v(lambda acc=acc: V.memset(acc[:, 16 + NW - NV - 1:16 + NW - NV], 0.0))
-        cmps = []
-        neq = None
-        for c in range(NV):
-            cut = 16 * c + 16
-            col = B("pw")[:, 16 * c + 15:16 * c + 16]
-            gname = "cmp%d_%d" % (r, c)
-            ts(fl[:, C * c:C * c + cut], bank(0, 0, cut), col, ALU.is_ge, 0.5, ALU.subtract, [pw], group=gname)
-            ts(fl[:, C * c + cut:C * c + C], bank(0, cut, C), col, ALU.is_gt, 0.5, ALU.subtract, [pw], group=gname)
-            cmps.append(gname)
-            if c == 0:
-                neq = scan(B("ne")[:], wide(2), B("eq")[:], 0.0, ALU.mult, ALU.subtract, [eq, w_a16])
-            else:
-                d = c - 1
-                scan(sb[:, H * d:H * d + H], fl[:, C * d:C * d + H], fl[:, C * d + H:C * d + C],
-                     B("ne")[:, 16 * d + 15:16 * d + 16], ALU.add, ALU.add, [cmps[d], neq], group="cnt%d" % r)
-        n = NW - NV
-        a1 = tt(acc[:, 32:32 + n], acc[:, 0:n], acc[:, 16:16 + n], ALU.add, ["acc%d" % r, nz])
-        d = NV - 1
-        scan(sb[:, H * d:H * d + H], fl[:, C * d:C * d + H], fl[:, C * d + H:C * d + C],
-             B("ne")[:, 16 * d + 15:16 * d + 16], ALU.add, ALU.add, [cmps[d], neq], group="cnt%d" % r)
-        a2 = ts(acc[:, 48:48 + n], acc[:, 32:32 + n], 0.5, ALU.mult, deps=[a1])
-        cnt = tt(sb[:, H * NV + H - 1:H * NW:H], acc[:, 48:48 + n], B("ne")[:, 16 * NV + 15:C:16], ALU.add, [a2, neq], group="cnt%d" % r)
-        i_w = ts(offs(0), sb[:, H - 1:H * NW:H], float(H), ALU.add, deps=[cnt])
+        pm, pw, nb, acc, ft, sb, sg = B("pm"), B("pw"), B("ne"), B("acc"), T.ft, T.sb, T.sg
+
+        def own(lo, hi):
+            return tt(pm[:, lo:hi], bank(0, lo, hi), T.wide[:, lo:hi], ALU.add, [w_own, p_v])
+
+        def hold(lo, hi, m):
+            return scan(pw[:, lo:hi], T.wide[:, C + lo:C + hi], pm[:, lo:hi], 0.0, ALU.add, ALU.min, [w_new, m])
+
+        def flags(c, n, step=4, first=0):
+            at = 4 * START[(c - 1) // 4] + (c - 1) % 4
+            return ft[:, at + first:at + 4 * n - 3:step]
+
+        def mine(c):
+            return pw[:, 16 * c + 15:16 * c + 16]
+
+        m_s = own(16 * S0, 16 * S1)
+        m_hi = own(16 * S1, C)
+        pw_s = hold(16 * S0, 16 * S1, m_s)
+        m_lo = own(0, 16 * S0)
+        pw_hi = hold(16 * S1, C, m_hi)
+        pw_lo = hold(0, 16 * S0, m_lo)
+        rows, signs = {}, []
+        clean = act(acc[:, 0:NW], t24, ACT.Copy, [it], scale=0.0)
+        for c in [4 * a + t for a in SCALAR_TILES for t in (4, 3, 2, 1)] + [None]:
+            if c:
+                signs.append((c, act(sg[:, C * c:C * c + 16 * c], bank(1, 0, 16 * c), ACT.Sign,
+                                     [p_s, pw_s if c >= S0 else pw_lo], bias=mine(c), scale=-1.0)))
+            if len(signs) == 2 or not c:
+                d, sign = signs.pop(0)
+                rows[d] = act(flags(d, 16 * d), sg[:, C * d:C * d + 16 * d], ACT.Sign,
+                              [clean, zero, sign], bias=0.5, scale=-1.0, accum_out=acc[:, d:d + 1])
+
+        def compare(a, held):
+            for c in range(min(4 * a + 4, NW - 1), 4 * a, -1):
+                rows[c] = ts(flags(c, 16 * c), bank(0, 0, 16 * c), mine(c), ALU.is_ge, 0.5, ALU.subtract, [zero, held],
+                             group="cmp%d_%d" % (r, a))
+
+        def add_up(cs):
+            for c in cs:
+                scan(sb[:, H * c + H - 8 * c:H * c + H], flags(c, 16 * c, 8), flags(c, 16 * c, 8, 4),
+                     nb[:, 16 * c + 15:16 * c + 16], ALU.add, ALU.add, [within, rows[c]], group="cnt%d" % r)
+
+        order = []
+
+        def pack(tiles):
+            lo, hi = START[tiles[0]], START[tiles[-1]] + max(128, WIDTH[tiles[-1]])
+            done = quant(T.qf[:, lo:hi], T.sf[:, lo:hi], ft[:, 4 * lo:4 * hi],
+                         [rows[c] for a in tiles for c in range(4 * a + 1, 4 * a + 5)])
+            for a in tiles:
+                k, n = 128 * (a in SCALAR_TILES), max(128, WIDTH[a])
+                order.append(a)
+                mm(6, n, T.qb[:, k:k + 128], T.sq[:, k:k + 128], T.qf[:, START[a]:START[a] + n],
+                   T.sf[:, START[a]:START[a] + n], [late["bd"]] + psum_free + [done],
+                   group="down%d" % r, start=len(order) == 1, stop=len(order) == NT)
+
+        compare(5, pw_hi)
+        rows[NW] = tt(flags(NW, C), bank(0, 0, C), pw[:], ALU.is_gt, [pw_s, pw_hi, pw_lo])
+        while soon:
+            soon.pop(0)()
+        if r == 0:
+            w_h16 = act(wide(2), small(3).indirect(T.cu[:, 0:NW]), ACT.Copy, [late["qo"], late["h16"]])
+            k_big = act(big16, col(42), ACT.Identity, [late["up"]], bias=1.0)
+            k_base = act(base, qcol, ACT.Identity, [pf], bias=H - 8.0)
+            k_sc = late["sc"]
+        fill_o = act(B("oc_")[:], T.jr[:], ACT.Copy, [c_jr], scale=0.0)
+        compare(2, pw_lo)
+        within = scan(nb[:], wide(0), flags(NW, C), 0.0, ALU.min, ALU.add, [rows[NW]])
+        pack([5])
+        within = cp(sb[:, H - 1:H * NW:H], nb[:, 15:C:16], [within])
+        compare(1, pw_lo)
+        pack([4])
+        add_up([23, 22, 21])
+        pack([2, 1])
+        add_up([12, 11])
+        pack([3])
+        add_up([10, 9, 8, 7, 6, 5])
+        pack([0])
+        by_v = ts(acc[:, 32:32 + NW], sb[:, H - 1:H * NW:H], big16, ALU.mult, deps=[k_big, "cnt%d" % r])
+        by_s = ts(acc[:, 64:64 + NW], acc[:, 0:NW], big16, ALU.mult, 0.5, ALU.mult, [rows[c] for c in range(1, NW)])
+        along = tt(acc[:, 32:32 + NW], acc[:, 32:32 + NW], acc[:, 64:64 + NW], ALU.add, [by_v, by_s])
+        h_c = scan(B("hc")[:], wide(2), bank(6, 0, C), 0.0, ALU.mult, ALU.add, [w_h16, "down%d" % r])
+        both = tt(acc[:, 0:NW], acc[:, 32:32 + NW], B("hc")[:, 15:C:16], ALU.subtract, [along, h_c])
+        i_w = ts(offs(0), acc[:, 0:NW], sc16, ALU.mult, base, ALU.add, [k_sc, k_base, both])
         remote(mate, B("li")[:], offs(0), "ai%d" % r, [i_w])
-        o_c = cp(B("oc_")[:].indirect(offs(0)), T.jc[:], [i_w, c_jc, fill])
-        if q_v is None:
-            q_v = quant(T.qv[:], T.sv[:], T.vt[:], [ld_v])
-        for b in range(4):
-            d_cp = act(B("dt")[:, b:4 * C:4], bank(2 + b, 0, C), ACT.Copy, [d_mm[b]], group="dcp%d" % r)
+        o_c = cp(B("oc_")[:].indirect(offs(0)), T.jc[:], [c_jc, fill_o, i_w])
+        fill_e = act(B("ec")[:], T.jr[:], ACT.Copy, scale=0.0)
 
         tab, hs, ka, kb = B("tab"), B("hs"), B("ka"), B("kb")
         came = ("ai%d" % r, ne)
 
         def wrap(src, k, dst, deps):
-            h = scan(part(hs, k), wide(3), src, 0.0, ALU.mult, ALU.add, deps + [w_h16])
-            return ts(dst, hs[:, C * k + 15:C * k + C:16], sc16, ALU.mult, float(H), ALU.add, [h, k_sc])
+            h = scan(part(hs, k), wide(2), src, 0.0, ALU.mult, ALU.add, deps)
+            return ts(dst, hs[:, C * k + 15:C * k + C:16], sc16, ALU.mult, float(H), ALU.add, [h])
 
-        t_k = act(part(tab, 0), B("oc_")[:].indirect(B("li")[:]), ACT.Copy, [o_c, came])
-        a_k = ts(part(ka, 0), B("oc_")[:].indirect(B("li")[:]), 512.0, ALU.mult, 512.0 * H + H, ALU.add, [o_c, came])
+        t_k = act(part(tab, 0), B("oc_")[:].indirect(B("li")[:]), ACT.Copy, [came, o_c])
+        a_k = ts(part(ka, 0), B("oc_")[:].indirect(B("li")[:]), KEY, ALU.mult, KEY * H + C, ALU.add, [came, o_c])
         b_k = act(part(kb, 0), part(ka, 0), ACT.Identity, [a_k], bias=-1.0)
         o_k = wrap(part(tab, 0), 0, offs(1), [t_k])
+        gap()
         for k in range(8):
             if k < 7:
                 t_n = act(part(tab, k + 1), part(tab, k).indirect(offs(k + 1)), ACT.Copy, [t_k, o_k])
             else:
                 b_last = act(part(kb, 8), part(ka, 7), ACT.Identity, [a_k], bias=-256.0)
-            a_n = tt(part(ka, k + 1), part(ka, k).indirect(offs(k + 1)), part(kb, k), ALU.min, [a_k, b_k, o_k])
+            a_n = tt(part(ka, k + 1), part(ka, k).indirect(offs(k + 1)), part(kb, k), ALU.min, [a_k, o_k, b_k])
             if k < 7:
                 b_k = act(part(kb, k + 1), part(ka, k + 1), ACT.Identity, [a_n], bias=-float(2 ** (k + 1)))
                 o_k = wrap(part(tab, k + 1), k + 1, offs(k + 2), [t_n])
                 t_k = t_n
+            gap()
             a_k = a_n
+        if r == 0:
+            w_h4 = act(wide(3), small(4).indirect(T.cu[:, NW:2 * NW]), ACT.Copy, [late["ro"], late["h4"]])
+            k_scm = act(scm, sc16, ACT.Copy, [k_sc], scale=1.0 / KEY)
+            k_sc4 = act(sc4, col(43), ACT.Copy, [late["s4"]], scale=4.0)
+            k_add4 = act(add4, rcol, ACT.Identity, [late["pg"]], bias=4.0 * H)
+        for b in range(4):
+            d_mm = mm(2 + b, C, T.qe[:, 128 * b:128 * b + 128], T.se[:, 128 * b:128 * b + 128], B("lq")[:], B("ls")[:],
+                      [late["qe"], ("aq%d" % r, 2 * ne)] + psum_free)
+            d_cp = act(B("dt")[:, b:4 * C:4], bank(2 + b, 0, C), ACT.Copy, [d_mm], group="dcp%d" % r)
         key = part(ka, 9)
-        a_k = tt(key, part(ka, 8).indirect(offs(8)), part(kb, 8), ALU.min, [a_k, b_last, o_k])
+        a_k = tt(key, part(ka, 8).indirect(offs(8)), part(kb, 8), ALU.min, [b_last, a_k])
         tl = B("tl")
-        h_m = scan(part(tl, 0), wide(3), key, 0.0, ALU.mult, ALU.add, [a_k, w_h16])
-        top = scan(part(tl, 1), key, key_i, -1.0e6, ALU.max, ALU.max, [a_k, c_i])
-        m1 = ts(acc[:, 0:NW], tl[:, 15:C:16], scm, ALU.mult, MAGIC, ALU.add, [h_m, k_scm, a1])
-        ends = scan(part(tl, 2), part(tl, 1), key_prev, -512.0 - 2 * H, ALU.add, ALU.subtract, [top])
-        m2 = ts(offs(9), acc[:, 0:NW], MAGIC, ALU.subtract, deps=[m1])
-        pos = tt(B("pc")[:], part(tl, 2).indirect(offs(9)), key, ALU.subtract, [ends, m2])
+        h_m = scan(part(tl, 0), wide(2), key, 0.0, ALU.mult, ALU.add, [a_k])
+        top = scan(part(tl, 1), key, key_i, -1.0e6, ALU.max, ALU.max, [c_i, a_k])
+        m_w = ts(offs(9), tl[:, 15:C:16], scm, ALU.mult, deps=[k_scm, h_m])
+        ends = scan(part(tl, 2), part(tl, 1), key_prev, -KEY - H, ALU.add, ALU.subtract, [top])
+        pos = tt(B("pc")[:], part(tl, 2).indirect(offs(9)), key, ALU.subtract, [m_w, ends])
         o_p = wrap(B("pc")[:], 8, offs(10), [pos])
-        e_c = cp(B("ec")[:].indirect(offs(10)), T.jc[:], [o_p, fill])
-        h_e = scan(part(hs, 9), wide(4), B("ec")[:], 0.0, ALU.mult, ALU.add, [e_c, w_h4])
+        e_c = cp(B("ec")[:].indirect(offs(10)), T.jc[:], [fill_e, o_p])
+        h_e = scan(part(hs, 9), wide(3), B("ec")[:], 0.0, ALU.mult, ALU.add, [w_h4, e_c])
         oe = B("oe")
-        o_e = ts(oe[:], hs[:, 9 * C + 3:10 * C:4], sc4, ALU.mult, add4, ALU.add, [h_e, k_sc4, k_add4])
+        o_e = ts(oe[:], hs[:, 9 * C + 3:10 * C:4], sc4, ALU.mult, add4, ALU.add, [k_sc4, k_add4, h_e])
         remote(mate, B("le")[:], oe[:, 0:NW], "ae%d" % r, [o_e])
 
         Z, zs, xs, qz, sz = B("z"), B("zs"), B("xs"), B("qz"), B("sz")
         Xn, qn, sn = T["x%d" % (r + 1)], T["qx%d" % (r + 1)], T["sx%d" % (r + 1)]
-        ga1 = cp(Z[:, 512:1024], X[:].indirect(oe[:, 32:64]), [o_e] + x_made)
-        ga2 = act(Z[:, 1024:1536], X[:].indirect(oe[:, 64:96]), ACT.Copy, [o_e] + x_made)
+        ga1 = cp(Z[:, 512:1024], X[:].indirect(oe[:, 32:64]), x_made + [o_e])
+        ga2 = act(Z[:, 1024:1536], X[:].indirect(oe[:, 64:96]), ACT.Copy, x_made + [o_e])
         q_a = quant(qz[:, 128:C], sz[:, 128:C], Z[:, 512:1536], [ga1, ga2])
         za2 = act(zs[:, 1024:1536], Z[:, 1024:1536], ACT.Copy, [ga2], scale=64.0)
         za1 = ts(zs[:, 512:1024], Z[:, 512:1024], 64.0, ALU.mult, deps=[ga1])
         gb1 = act(Z[:, 384:512], X[:].indirect(oe[:, 24:32]), ACT.Copy, [o_e])
         gb2 = act(Z[:, 0:384], B("dt")[:].indirect(B("le")[:]), ACT.Copy, [d_cp, ("ae%d" % r, ne)])
-        zb = act(zs[:, 0:512], Z[:, 0:512], ACT.Copy, [gb1, gb2], scale=64.0)
-        if r == R - 1:
-            e_f = act(T.ef[:], B("ec")[:], ACT.Identity, [e_c], bias=float(H))
-            st_e = dma("y", T.el[:], T.ef[0:128:16, :], [e_f], group="st")
 
         def wb(b):
             return T.qw[:, 128 * b:128 * b + 128], T.sw[:, 128 * b:128 * b + 128]
 
-        m_a = [mm(b, 256, wb(b)[0], wb(b)[1], qz[:, 128:C], sz[:, 128:C], [q_a, ld_w, d_cp, cnt]) for b in range(4)]
-        for b in range(4):
-            r_a = tt(xs[:, 512 + b:1536:4], bank(b, 0, 256), zs[:, 512 + b:1536:4], ALU.add, [m_a[b], za1, za2], group="ra%d" % r)
+        m_a = [mm(b, 256, wb(b)[0], wb(b)[1], qz[:, 128:C], sz[:, 128:C], [ld_w, d_cp, q_a]) for b in range(4)]
+        r_a = [tt(xs[:, 512 + b:1536:4], bank(b, 0, 256), zs[:, 512 + b:1536:4], ALU.add, [za1, za2, m_a[b]]) for b in range(4)]
         q_b = quant(qz[:, 0:128], sz[:, 0:128], Z[:, 0:512], [gb1, gb2])
         m_b = [mm(4 + b, 128, wb(b)[0], wb(b)[1], qz[:, 0:128], sz[:, 0:128], [q_b]) for b in range(4)]
-        x_a = ts(Xn[:, 512:1536], xs[:, 512:1536], 0.015625, ALU.mult, deps=[r_a])
+        zb = ts(zs[:, 0:512], Z[:, 0:512], 64.0, ALU.mult, deps=[gb1, gb2])
+        x_a = act(Xn[:, 512:1536], xs[:, 512:1536], ACT.Copy, r_a, scale=0.015625)
         for b in range(4):
-            r_b = tt(xs[:, b:512:4], bank(4 + b, 0, 128), zs[:, b:512:4], ALU.add, [m_b[b], zb], group="rb%d" % r)
-        n_a = quant(qn[:, 128:C], sn[:, 128:C], Xn[:, 512:1536], [x_a])
+            r_b = tt(xs[:, b:512:4], bank(4 + b, 0, 128), zs[:, b:512:4], ALU.add, [zb, m_b[b]], group="rb%d" % r)
+        if r == R - 1:
+            e_f = act(T.ef[:], B("ec")[:], ACT.Identity, [e_c], bias=float(H))
+            dma("y", T.el[:], T.ef[0:128:16, :], [e_f], group="st")
         x_b = ts(Xn[:, 0:512], xs[:, 0:512], 0.015625, ALU.mult, deps=[r_b])
+        n_a = quant(qn[:, 128:C], sn[:, 128:C], Xn[:, 512:1536], [x_a])
         n_b = quant(qn[:, 0:128], sn[:, 0:128], Xn[:, 0:512], [x_b])
-        q_x, x_made, psum_free = [n_a, n_b], [x_a, x_b], [r_a, r_b]
+        q_x, x_made, psum_free = [n_a, n_b], [x_a, x_b], r_a + [r_b]
 
     qn, sn = T["qx%d" % R], T["sx%d" % R]
-    y_a = mm(0, 256, T.qv[:], T.sv[:], qn[:, 128:C], sn[:, 128:C], [q_x[0], q_v, psum_free[0]])
-    y_b = mm(1, 128, T.qv[:], T.sv[:], qn[:, 0:128], sn[:, 0:128], [q_x[1]])
+    y_a = mm(0, 256, T.qv[:], T.sv[:], qn[:, 128:C], sn[:, 128:C], [late["qv"]] + psum_free[:1] + [q_x[0]])
+    y_b = mm(1, 128, T.qv[:], T.sv[:], qn[:, 0:128], sn[:, 0:128], psum_free[1:2] + [q_x[1]])
     dma("y", T.oc[:, 512:1536], qn[:, 128:C].bitcast(dt.uint8), [q_x[0]], group="st")
     c_a = act(T.yt[:, 128:C], bank(0, 0, 256), ACT.Copy, [y_a])
     dma("s", T.y[:, 128:C], T.yt[:, 128:C], [c_a], group="st")

@@ -369,23 +369,29 @@ def rank_program(g, core, T, topo):
             h = scan(part(hs, k), wide(2), src, 0.0, ALU.mult, ALU.add, deps)
             return ts(dst, hs[:, C * k + 15:C * k + C:16], sc16, ALU.mult, float(H), ALU.add, [h])
 
-        t_k = act(part(tab, 0), B("oc_")[:].indirect(B("li")[:]), ACT.Copy, [came, o_c])
-        a_k = ts(part(ka, 0), B("oc_")[:].indirect(B("li")[:]), KEY, ALU.mult, KEY * H + C, ALU.add, [came, o_c])
-        b_k = act(part(kb, 0), part(ka, 0), ACT.Identity, [a_k], bias=-1.0)
-        o_k = wrap(part(tab, 0), 0, offs(1), [t_k])
-        gap()
+        def half(buf, k, h):
+            return buf[:, C * k + H * h:C * k + H * h + H]
+
+        def list_half(tile, k, h):
+            return tile[:, NW * k + NW // 2 * h:NW * k + NW // 2 * (h + 1)]
+
+        a_k = [ts(half(ka, 0, h), B("oc_")[:].indirect(list_half(B("li"), 0, h)), KEY, ALU.mult, KEY * H + C, ALU.add,
+                  [came, o_c]) for h in range(2)]
+        t_k, o_k = [came, o_c], [None, None]
         for k in range(8):
-            if k < 7:
-                t_n = act(part(tab, k + 1), part(tab, k).indirect(offs(k + 1)), ACT.Copy, [t_k, o_k])
-            else:
-                b_last = act(part(kb, 8), part(ka, 7), ACT.Identity, [a_k], bias=-256.0)
-            a_n = tt(part(ka, k + 1), part(ka, k).indirect(offs(k + 1)), part(kb, k), ALU.min, [a_k, o_k, b_k])
-            if k < 7:
-                b_k = act(part(kb, k + 1), part(ka, k + 1), ACT.Identity, [a_n], bias=-float(2 ** (k + 1)))
-                o_k = wrap(part(tab, k + 1), k + 1, offs(k + 2), [t_n])
-                t_k = t_n
+            src, lst = (part(tab, k - 1), off) if k else (B("oc_")[:], B("li"))
+            t_k = [act(half(tab, k, h), (part(tab, k - 1) if k else B("oc_")[:]).indirect(list_half(lst, k, h)), ACT.Copy,
+                       t_k + [o_k[h]]) for h in range(2)]
+            b_k = [act(half(kb, k, h), half(ka, k, h), ACT.Identity, [a_k[h]], bias=-float(2 ** k)) for h in range(2)]
+            h_k = [scan(half(hs, k, h), T.wide[:, 2 * C:2 * C + H], half(tab, k, h), 0.0, ALU.mult, ALU.add, [t_k[h]])
+                   for h in range(2)]
+            o_k = [ts(list_half(off, k + 1, h), hs[:, C * k + H * h + 15:C * k + H * h + H:16], sc16, ALU.mult,
+                      float(H), ALU.add, [h_k[h]]) for h in range(2)]
+            a_k = [tt(half(ka, k + 1, h), part(ka, k).indirect(list_half(off, k + 1, h)), half(kb, k, h), ALU.min,
+                      a_k + [o_k[h], b_k[h]]) for h in range(2)]
             gap()
-            a_k = a_n
+        b_last = act(part(kb, 8), part(ka, 7), ACT.Identity, b_k, bias=-256.0)
+        gap()
         if r == 0:
             w_h4 = act(wide(3), small(4).indirect(T.cu[:, NW:2 * NW]), ACT.Copy, [late["ro"], late["h4"]])
             k_scm = act(scm, sc16, ACT.Copy, [k_sc], scale=1.0 / KEY)
@@ -396,7 +402,7 @@ def rank_program(g, core, T, topo):
                       [late["qe"], ("aq%d" % r, 2 * ne)] + psum_free)
             d_cp = act(B("dt")[:, b:4 * C:4], bank(2 + b, 0, C), ACT.Copy, [d_mm], group="dcp%d" % r)
         key = part(ka, 9)
-        a_k = tt(key, part(ka, 8).indirect(offs(8)), part(kb, 8), ALU.min, [b_last, a_k])
+        a_k = tt(key, part(ka, 8).indirect(offs(8)), part(kb, 8), ALU.min, [b_last] + a_k)
         tl = B("tl")
         h_m = scan(part(tl, 0), wide(2), key, 0.0, ALU.mult, ALU.add, [a_k])
         top = scan(part(tl, 1), key, key_i, -1.0e6, ALU.max, ALU.max, [c_i, a_k])

@@ -5,7 +5,7 @@ ACT = ActivationFunctionType
 C, S, R = 384, 96, 2
 STEP = [2, 1]
 NW = C // 16
-S0, S1 = 13, 21
+S0, S1 = 14, 21
 NT = NW // 4
 BIG = 2.0 ** 40
 FAR = 2.0 ** 96
@@ -15,7 +15,13 @@ X4, U8, BF, F32, U16, I32 = "float8_e4m3fn_x4", "uint8", "bfloat16", "float32", 
 WIDTH = [64 * a + 64 for a in range(NT)]
 START = [sum(WIDTH[a + 1:]) for a in range(NT)]
 WORDS = sum(WIDTH) + 64
-SCALAR_TILES = [4, 3, 0]
+
+
+def weights(a):
+    return tuple(0.5 if S0 <= c < S1 else 1.0 for c in range(4 * a + 1, 4 * a + 5))
+
+
+KINDS = sorted(set(weights(a) for a in range(NT)), reverse=True)
 
 SCRATCH = {
     "ps": ("psum", [128, 4096], F32),
@@ -26,7 +32,8 @@ SCRATCH = {
     "qw": ("sbuf", [128, 512], X4), "sw": ("sbuf", [128, 512], U8),
     "ones": ("sbuf", [128, 528], BF), "et": ("sbuf", [128, 528], BF),
     "qe": ("sbuf", [128, 512], X4), "se": ("sbuf", [128, 512], U8),
-    "bw": ("sbuf", [128, 1024], BF), "qb": ("sbuf", [128, 256], X4), "sq": ("sbuf", [128, 256], U8),
+    "bw": ("sbuf", [128, 512 * len(KINDS)], BF),
+    "qb": ("sbuf", [128, 128 * len(KINDS)], X4), "sq": ("sbuf", [128, 128 * len(KINDS)], U8),
     "ci": ("sbuf", [128, 64], I32), "cf": ("sbuf", [128, 64], F32), "cs": ("sbuf", [128, 160], BF),
     "cu": ("sbuf", [128, 96], U16),
     "wide": ("sbuf", [128, 4 * C], BF), "jr": ("sbuf", [128, C], BF), "jc": ("sbuf", [128, C], BF),
@@ -215,17 +222,17 @@ def rank_program(g, core, T, topo):
     k_a16 = ts(small(2), t16, qcol, ALU.is_gt, deps=[it, pf])
     k_c16 = ts(small(8), less1, qcol, ALU.is_equal, BIG, ALU.mult, [it, pf])
     c_bd = act(T.bw[:, 0:512], small(0).indirect(T.cu[:, 56:88]), ACT.Copy, [uo, k_grp])
-    c_bw = act(T.bw[:, 512:1024], T.bw[:, 0:512], ACT.Copy, [c_bd], scale=0.5)
+    for k, w in list(enumerate(KINDS))[1:]:
+        for t, step in ([(0, 1)] if len(set(w)) == 1 else [(t, 4) for t in range(4)]):
+            c_bw = act(T.bw[:, 512 * k + t:512 * k + 512:step], T.bw[:, t:512:step], ACT.Copy, [c_bd], group="bw", scale=w[t])
     x_made = list(ld_x)
     psum_free = []
     late = {}
-    soon = [
-        lambda: late.update(h16=tt(small(3), small(8), small(2), ALU.max, [k_a16, k_c16])),
-        lambda: late.update(qo=ts(T.cu[:, 0:NW], t24, 0.0, ALU.mult, qcol, ALU.add, [it, pf])),
-        lambda: late.update(sc=ts(sc16, qcol, 15.0, ALU.is_equal, 1.0 / BIG, ALU.max, [pf])),
-        lambda: late.update(up=ts(col(42), qcol, 15.0, ALU.is_lt, BIG, ALU.mult, [pf])),
-        lambda: late.update(bd=quant(T.qb[:], T.sq[:], T.bw[:], [c_bw])),
-    ]
+    late["qo"] = ts(T.cu[:, 0:NW], t24, 0.0, ALU.mult, qcol, ALU.add, [it, pf])
+    late["sc"] = ts(sc16, qcol, 15.0, ALU.is_equal, 1.0 / BIG, ALU.max, [pf])
+    late["up"] = ts(col(42), qcol, 15.0, ALU.is_lt, BIG, ALU.mult, [pf])
+    late["h16"] = tt(small(3), small(8), small(2), ALU.max, [k_a16, k_c16])
+    late["bd"] = quant(T.qb[:], T.sq[:], T.bw[:], [c_bw])
 
     def unpacker(b):
         return lambda: late.update(qe=quant(T.qe[:, 128 * b:128 * b + 128], T.se[:, 128 * b:128 * b + 128],
@@ -273,7 +280,6 @@ def rank_program(g, core, T, topo):
             c_jc = gp(lambda: g.iota(T.jc[:], [[1, C]], -H, 0, **fl_ok))
             late["et"] = gp(lambda: g.affine_select(T.et[:], T.ones[:], [[-1, 528]], ALU.is_equal, 0.0, 3, 4), [one])
             c_i = gp(lambda: g.iota(T.iall[:], [[int(KEY), C + 8]], -int(KEY), 0, **fl_ok))
-        key_i, key_prev = T.iall[:, 1:C + 1], T.iall[:, 0:C]
 
         pm, pw, nb, acc, ft, sb, sg = B("pm"), B("pw"), B("ne"), B("acc"), T.ft, T.sb, T.sg
 
@@ -290,25 +296,23 @@ def rank_program(g, core, T, topo):
         def mine(c):
             return pw[:, 16 * c + 15:16 * c + 16]
 
-        m_s = own(16 * S0, 16 * S1)
-        m_hi = own(16 * S1, C)
-        pw_s = hold(16 * S0, 16 * S1, m_s)
-        m_lo = own(0, 16 * S0)
-        pw_hi = hold(16 * S1, C, m_hi)
-        pw_lo = hold(0, 16 * S0, m_lo)
+        m_s, m_hi, m_lo = own(16 * S0, 16 * S1), own(16 * S1, C), own(0, 16 * S0)
+        pw_s, pw_hi, pw_lo = hold(16 * S0, 16 * S1, m_s), hold(16 * S1, C, m_hi), hold(0, 16 * S0, m_lo)
         rows, signs = {}, []
-        clean = act(acc[:, 0:NW], t24, ACT.Copy, [it], scale=0.0)
-        for c in [4 * a + t for a in SCALAR_TILES for t in (4, 3, 2, 1)] + [None]:
+        for c in list(range(S1 - 1, S0 - 1, -1)) + [None]:
             if c:
                 signs.append((c, act(sg[:, C * c:C * c + 16 * c], bank(1, 0, 16 * c), ACT.Sign,
-                                     [p_s, pw_s if c >= S0 else pw_lo], bias=mine(c), scale=-1.0)))
+                                     [p_s, pw_s], bias=mine(c), scale=-1.0)))
             if len(signs) == 2 or not c:
                 d, sign = signs.pop(0)
                 rows[d] = act(flags(d, 16 * d), sg[:, C * d:C * d + 16 * d], ACT.Sign,
-                              [clean, zero, sign], bias=0.5, scale=-1.0, accum_out=acc[:, d:d + 1])
+                              [zero, sign], bias=0.5, scale=-1.0, accum_out=acc[:, d:d + 1])
+
+        def mine_v(a):
+            return [c for c in range(min(4 * a + 4, NW - 1), 4 * a, -1) if not S0 <= c < S1]
 
         def compare(a, held):
-            for c in range(min(4 * a + 4, NW - 1), 4 * a, -1):
+            for c in mine_v(a):
                 rows[c] = ts(flags(c, 16 * c), bank(0, 0, 16 * c), mine(c), ALU.is_ge, 0.5, ALU.subtract, [zero, held],
                              group="cmp%d_%d" % (r, a))
 
@@ -324,7 +328,7 @@ def rank_program(g, core, T, topo):
             done = quant(T.qf[:, lo:hi], T.sf[:, lo:hi], ft[:, 4 * lo:4 * hi],
                          [rows[c] for a in tiles for c in range(4 * a + 1, 4 * a + 5)])
             for a in tiles:
-                k, n = 128 * (a in SCALAR_TILES), max(128, WIDTH[a])
+                k, n = 128 * KINDS.index(weights(a)), max(128, WIDTH[a])
                 order.append(a)
                 mm(6, n, T.qb[:, k:k + 128], T.sq[:, k:k + 128], T.qf[:, START[a]:START[a] + n],
                    T.sf[:, START[a]:START[a] + n], [late["bd"]] + psum_free + [done],
@@ -332,31 +336,32 @@ def rank_program(g, core, T, topo):
 
         compare(5, pw_hi)
         rows[NW] = tt(flags(NW, C), bank(0, 0, C), pw[:], ALU.is_gt, [pw_s, pw_hi, pw_lo])
-        while soon:
-            soon.pop(0)()
         if r == 0:
             w_h16 = act(wide(2), small(3).indirect(T.cu[:, 0:NW]), ACT.Copy, [late["qo"], late["h16"]])
             k_big = act(big16, col(42), ACT.Identity, [late["up"]], bias=1.0)
             k_base = act(base, qcol, ACT.Identity, [pf], bias=H - 8.0)
             k_sc = late["sc"]
         fill_o = act(B("oc_")[:], T.jr[:], ACT.Copy, [c_jr], scale=0.0)
+        compare(3, pw_lo)
         compare(2, pw_lo)
         within = scan(nb[:], wide(0), flags(NW, C), 0.0, ALU.min, ALU.add, [rows[NW]])
         pack([5])
-        within = cp(sb[:, H - 1:H * NW:H], nb[:, 15:C:16], [within])
+        cp(sb[:, H - 1:H], nb[:, 15:16], [within], group="cnt%d" % r)
         compare(1, pw_lo)
+        compare(0, pw_lo)
         pack([4])
-        add_up([23, 22, 21])
-        pack([2, 1])
-        add_up([12, 11])
+        add_up(mine_v(5))
+        pack([2, 1, 0])
+        add_up(mine_v(3) + mine_v(2))
         pack([3])
-        add_up([10, 9, 8, 7, 6, 5])
-        pack([0])
-        by_v = ts(acc[:, 32:32 + NW], sb[:, H - 1:H * NW:H], big16, ALU.mult, deps=[k_big, "cnt%d" % r])
-        by_s = ts(acc[:, 64:64 + NW], acc[:, 0:NW], big16, ALU.mult, 0.5, ALU.mult, [rows[c] for c in range(1, NW)])
-        along = tt(acc[:, 32:32 + NW], acc[:, 32:32 + NW], acc[:, 64:64 + NW], ALU.add, [by_v, by_s])
+        by_s = ts(acc[:, 64 + S0:64 + S1], acc[:, S0:S1], 0.5, ALU.mult, deps=[rows[c] for c in range(S0, S1)])
+        add_up(mine_v(1))
+        tt(sb[:, H * S0 + H - 1:H * S1:H], acc[:, 64 + S0:64 + S1], nb[:, 16 * S0 + 15:16 * S1:16], ALU.add, [within, by_s],
+           group="cnt%d" % r)
+        add_up(mine_v(0))
         h_c = scan(B("hc")[:], wide(2), bank(6, 0, C), 0.0, ALU.mult, ALU.add, [w_h16, "down%d" % r])
-        both = tt(acc[:, 0:NW], acc[:, 32:32 + NW], B("hc")[:, 15:C:16], ALU.subtract, [along, h_c])
+        along = ts(acc[:, 32:32 + NW], sb[:, H - 1:H * NW:H], big16, ALU.mult, deps=[k_big, "cnt%d" % r])
+        both = tt(acc[:, 0:NW], acc[:, 32:32 + NW], B("hc")[:, 15:C:16], ALU.subtract, [h_c, along])
         i_w = ts(offs(0), acc[:, 0:NW], sc16, ALU.mult, base, ALU.add, [k_sc, k_base, both])
         remote(mate, B("li")[:], offs(0), "ai%d" % r, [i_w])
         o_c = cp(B("oc_")[:].indirect(offs(0)), T.jc[:], [c_jc, fill_o, i_w])
@@ -365,9 +370,7 @@ def rank_program(g, core, T, topo):
         tab, hs, ka, kb = B("tab"), B("hs"), B("ka"), B("kb")
         came = ("ai%d" % r, ne)
 
-        def wrap(src, k, dst, deps):
-            h = scan(part(hs, k), wide(2), src, 0.0, ALU.mult, ALU.add, deps)
-            return ts(dst, hs[:, C * k + 15:C * k + C:16], sc16, ALU.mult, float(H), ALU.add, [h])
+        w_half = T.wide[:, 2 * C:2 * C + H]
 
         def half(buf, k, h):
             return buf[:, C * k + H * h:C * k + H * h + H]
@@ -375,18 +378,20 @@ def rank_program(g, core, T, topo):
         def list_half(tile, k, h):
             return tile[:, NW * k + NW // 2 * h:NW * k + NW // 2 * (h + 1)]
 
+        def wrap(src, k, via, to, made):
+            lifted = [scan(half(hs, via, h), w_half, half(src, k, h), 0.0, ALU.mult, ALU.add, [made[h]]) for h in range(2)]
+            return [ts(list_half(off, to, h), hs[:, C * via + H * h + 15:C * via + H * h + H:16], sc16, ALU.mult,
+                       float(H), ALU.add, [lifted[h]]) for h in range(2)]
+
         a_k = [ts(half(ka, 0, h), B("oc_")[:].indirect(list_half(B("li"), 0, h)), KEY, ALU.mult, KEY * H + C, ALU.add,
                   [came, o_c]) for h in range(2)]
         t_k, o_k = [came, o_c], [None, None]
         for k in range(8):
-            src, lst = (part(tab, k - 1), off) if k else (B("oc_")[:], B("li"))
+            lst = off if k else B("li")
             t_k = [act(half(tab, k, h), (part(tab, k - 1) if k else B("oc_")[:]).indirect(list_half(lst, k, h)), ACT.Copy,
                        t_k + [o_k[h]]) for h in range(2)]
             b_k = [act(half(kb, k, h), half(ka, k, h), ACT.Identity, [a_k[h]], bias=-float(2 ** k)) for h in range(2)]
-            h_k = [scan(half(hs, k, h), T.wide[:, 2 * C:2 * C + H], half(tab, k, h), 0.0, ALU.mult, ALU.add, [t_k[h]])
-                   for h in range(2)]
-            o_k = [ts(list_half(off, k + 1, h), hs[:, C * k + H * h + 15:C * k + H * h + H:16], sc16, ALU.mult,
-                      float(H), ALU.add, [h_k[h]]) for h in range(2)]
+            o_k = wrap(tab, k, k, k + 1, t_k)
             a_k = [tt(half(ka, k + 1, h), part(ka, k).indirect(list_half(off, k + 1, h)), half(kb, k, h), ALU.min,
                       a_k + [o_k[h], b_k[h]]) for h in range(2)]
             gap()
@@ -401,61 +406,92 @@ def rank_program(g, core, T, topo):
             d_mm = mm(2 + b, C, T.qe[:, 128 * b:128 * b + 128], T.se[:, 128 * b:128 * b + 128], B("lq")[:], B("ls")[:],
                       [late["qe"], ("aq%d" % r, 2 * ne)] + psum_free)
             d_cp = act(B("dt")[:, b:4 * C:4], bank(2 + b, 0, C), ACT.Copy, [d_mm], group="dcp%d" % r)
-        key = part(ka, 9)
-        a_k = tt(key, part(ka, 8).indirect(offs(8)), part(kb, 8), ALU.min, [b_last] + a_k)
-        tl = B("tl")
-        h_m = scan(part(tl, 0), wide(2), key, 0.0, ALU.mult, ALU.add, [a_k])
-        top = scan(part(tl, 1), key, key_i, -1.0e6, ALU.max, ALU.max, [c_i, a_k])
-        m_w = ts(offs(9), tl[:, 15:C:16], scm, ALU.mult, deps=[k_scm, h_m])
-        ends = scan(part(tl, 2), part(tl, 1), key_prev, -KEY - H, ALU.add, ALU.subtract, [top])
-        pos = tt(B("pc")[:], part(tl, 2).indirect(offs(9)), key, ALU.subtract, [m_w, ends])
-        o_p = wrap(B("pc")[:], 8, offs(10), [pos])
-        e_c = cp(B("ec")[:].indirect(offs(10)), T.jc[:], [fill_e, o_p])
-        h_e = scan(part(hs, 9), wide(3), B("ec")[:], 0.0, ALU.mult, ALU.add, [w_h4, e_c])
-        oe = B("oe")
-        o_e = ts(oe[:], hs[:, 9 * C + 3:10 * C:4], sc4, ALU.mult, add4, ALU.add, [k_sc4, k_add4, h_e])
-        remote(mate, B("le")[:], oe[:, 0:NW], "ae%d" % r, [o_e])
+        tl, pc, oe = B("tl"), B("pc"), B("oe")
+        a_k = [tt(half(ka, 9, h), part(ka, 8).indirect(list_half(off, 8, h)), half(kb, 8, h), ALU.min, [b_last] + a_k)
+               for h in range(2)]
+        top, h_m = [], []
+        for h in range(2):
+            top.append(scan(half(tl, 1, h), half(ka, 9, h), T.iall[:, 1 + H * h:1 + H * h + H], -1.0e6, ALU.max, ALU.max,
+                            [c_i, a_k[h]]))
+            h_m.append(scan(half(tl, 0, h), w_half, half(ka, 9, h), 0.0, ALU.mult, ALU.add, [a_k[h]]))
+        ends = scan(part(tl, 2), part(tl, 1), T.iall[:, 0:C], -KEY - H, ALU.add, ALU.subtract, top)
+        m_w = ts(offs(9), tl[:, 15:C:16], scm, ALU.mult, deps=[k_scm] + h_m)
+        pos = [tt(half(pc, 0, h), part(tl, 2).indirect(list_half(off, 9, h)), half(ka, 9, h), ALU.subtract, [ends, m_w])
+               for h in range(2)]
+        o_p = wrap(pc, 0, 8, 10, pos)
+        e_c = cp(B("ec")[:].indirect(offs(10)), T.jc[:], [fill_e] + o_p)
+        cuts = [(0, 128), (128, C)]
+        h_e = [scan(hs[:, 9 * C + lo:9 * C + hi], T.wide[:, 3 * C + lo:3 * C + hi], B("ec")[:, lo:hi], 0.0, ALU.mult, ALU.add,
+                    [w_h4, e_c]) for lo, hi in cuts]
+        o_e = [ts(oe[:, lo // 4:hi // 4], hs[:, 9 * C + lo + 3:9 * C + hi:4], sc4, ALU.mult, add4, ALU.add,
+                  [k_sc4, k_add4, h_e[k]]) for k, (lo, hi) in enumerate(cuts)]
+        remote(mate, B("le")[:], oe[:, 0:NW], "ae%d" % r, [o_e[0]])
 
         Z, zs, xs, qz, sz = B("z"), B("zs"), B("xs"), B("qz"), B("sz")
         Xn, qn, sn = T["x%d" % (r + 1)], T["qx%d" % (r + 1)], T["sx%d" % (r + 1)]
-        ga1 = cp(Z[:, 512:1024], X[:].indirect(oe[:, 32:64]), x_made + [o_e])
-        ga2 = act(Z[:, 1024:1536], X[:].indirect(oe[:, 64:96]), ACT.Copy, x_made + [o_e])
-        q_a = quant(qz[:, 128:C], sz[:, 128:C], Z[:, 512:1536], [ga1, ga2])
-        za2 = act(zs[:, 1024:1536], Z[:, 1024:1536], ACT.Copy, [ga2], scale=64.0)
-        za1 = ts(zs[:, 512:1024], Z[:, 512:1024], 64.0, ALU.mult, deps=[ga1])
-        gb1 = act(Z[:, 384:512], X[:].indirect(oe[:, 24:32]), ACT.Copy, [o_e])
-        gb2 = act(Z[:, 0:384], B("dt")[:].indirect(B("le")[:]), ACT.Copy, [d_cp, ("ae%d" % r, ne)])
+        free = [[] for b in range(8)]
 
-        def wb(b):
-            return T.qw[:, 128 * b:128 * b + 128], T.sw[:, 128 * b:128 * b + 128]
+        def pick(by, lo, hi, src, lst, deps):
+            out, in_ = Z[:, 4 * lo:4 * hi], src[:].indirect(lst[:, lo // 4:hi // 4])
+            return cp(out, in_, deps) if by == "v" else act(out, in_, ACT.Copy, deps)
 
-        m_a = [mm(b, 256, wb(b)[0], wb(b)[1], qz[:, 128:C], sz[:, 128:C], [ld_w, d_cp, q_a]) for b in range(4)]
-        r_a = [tt(xs[:, 512 + b:1536:4], bank(b, 0, 256), zs[:, 512 + b:1536:4], ALU.add, [za1, za2, m_a[b]]) for b in range(4)]
-        q_b = quant(qz[:, 0:128], sz[:, 0:128], Z[:, 0:512], [gb1, gb2])
-        m_b = [mm(4 + b, 128, wb(b)[0], wb(b)[1], qz[:, 0:128], sz[:, 0:128], [q_b]) for b in range(4)]
-        zb = ts(zs[:, 0:512], Z[:, 0:512], 64.0, ALU.mult, deps=[gb1, gb2])
-        x_a = act(Xn[:, 512:1536], xs[:, 512:1536], ACT.Copy, r_a, scale=0.015625)
-        for b in range(4):
-            r_b = tt(xs[:, b:512:4], bank(4 + b, 0, 128), zs[:, b:512:4], ALU.add, [zb, m_b[b]], group="rb%d" % r)
+        def scaled(by, out, in_, lo, hi, c, deps):
+            if by == "v":
+                return ts(out[:, 4 * lo:4 * hi], in_[:, 4 * lo:4 * hi], c, ALU.mult, deps=deps)
+            return act(out[:, 4 * lo:4 * hi], in_[:, 4 * lo:4 * hi], ACT.Copy, deps, scale=c)
+
+        def products(lo, first, deps):
+            done = quant(qz[:, lo:lo + 128], sz[:, lo:lo + 128], Z[:, 4 * lo:4 * lo + 512], deps)
+            return [mm(first + b, 128, T.qw[:, 128 * b:128 * b + 128], T.sw[:, 128 * b:128 * b + 128], qz[:, lo:lo + 128],
+                       sz[:, lo:lo + 128], [ld_w, d_cp] + free[first + b] + [done]) for b in range(4)]
+
+        def sums(lo, first, made, deps, bs=range(4)):
+            for b in bs:
+                free[first + b] = [tt(xs[:, 4 * lo + b:4 * lo + 512:4], bank(first + b, 0, 128),
+                                      zs[:, 4 * lo + b:4 * lo + 512:4], ALU.add, deps + [made[b]])]
+            return [free[first + b][0] for b in bs]
+
+        def state(lo, deps):
+            return quant(qn[:, lo:lo + 128], sn[:, lo:lo + 128], Xn[:, 4 * lo:4 * lo + 512], deps)
+
+        listed = x_made + [o_e[1]]
+        g_b = [pick("s", 96, 128, X, oe, x_made + [o_e[0]])]
+        g_1 = [pick("v", 128, 192, X, oe, listed), pick("s", 192, 256, X, oe, listed)]
+        g_2 = [pick("v", 256, 320, X, oe, listed), pick("s", 320, 384, X, oe, listed)]
         if r == R - 1:
             e_f = act(T.ef[:], B("ec")[:], ACT.Identity, [e_c], bias=float(H))
             dma("y", T.el[:], T.ef[0:128:16, :], [e_f], group="st")
-        x_b = ts(Xn[:, 0:512], xs[:, 0:512], 0.015625, ALU.mult, deps=[r_b])
-        n_a = quant(qn[:, 128:C], sn[:, 128:C], Xn[:, 512:1536], [x_a])
-        n_b = quant(qn[:, 0:128], sn[:, 0:128], Xn[:, 0:512], [x_b])
-        q_x, x_made, psum_free = [n_a, n_b], [x_a, x_b], r_a + [r_b]
+        m_1 = products(128, 0, g_1)
+        z_1 = scaled("v", zs, Z, 128, 256, 64.0, g_1)
+        m_2 = products(256, 4, g_2)
+        z_2 = scaled("v", zs, Z, 256, 384, 64.0, g_2)
+        g_b.append(pick("s", 0, S, B("dt"), B("le"), [d_cp, ("ae%d" % r, ne)]))
+        r_1 = sums(128, 0, m_1, [z_1])
+        r_2 = sums(256, 4, m_2, [z_2], (0, 1))
+        m_b = products(0, 0, g_b)
+        z_b = scaled("s", zs, Z, 0, 128, 64.0, g_b)
+        r_2 += sums(256, 4, m_2, [z_2], (2, 3))
+        x_1 = scaled("v", Xn, xs, 128, 256, 0.015625, r_1)
+        x_2 = scaled("s", Xn, xs, 256, 384, 0.015625, r_2)
+        r_b = sums(0, 0, m_b, [z_b])
+        n_1 = state(128, [x_1])
+        n_2 = state(256, [x_2])
+        x_b = [scaled("v", Xn, xs, 0, 88, 0.015625, r_b), scaled("s", Xn, xs, 88, 128, 0.015625, r_b)]
+        n_b = state(0, x_b)
+        q_x, x_made, psum_free = [n_1, n_2, n_b], [x_1, x_2] + x_b, r_2 + r_b
 
     qn, sn = T["qx%d" % R], T["sx%d" % R]
-    y_a = mm(0, 256, T.qv[:], T.sv[:], qn[:, 128:C], sn[:, 128:C], [late["qv"]] + psum_free[:1] + [q_x[0]])
-    y_b = mm(1, 128, T.qv[:], T.sv[:], qn[:, 0:128], sn[:, 0:128], psum_free[1:2] + [q_x[1]])
-    dma("y", T.oc[:, 512:1536], qn[:, 128:C].bitcast(dt.uint8), [q_x[0]], group="st")
-    c_a = act(T.yt[:, 128:C], bank(0, 0, 256), ACT.Copy, [y_a])
-    dma("s", T.y[:, 128:C], T.yt[:, 128:C], [c_a], group="st")
-    c_b = cp(T.yt[:, 0:128], bank(1, 0, 128), [y_b])
-    dma("y", T.oc[:, 0:512], qn[:, 0:128].bitcast(dt.uint8), [q_x[1]], group="st")
+    for k, lo in enumerate((128, 256, 0)):
+        y_k = mm(4 + k, 128, T.qv[:], T.sv[:], qn[:, lo:lo + 128], sn[:, lo:lo + 128], [late["qv"]] + r_2 + [q_x[k]])
+        dma("y", T.oc[:, 4 * lo:4 * lo + 512], qn[:, lo:lo + 128].bitcast(dt.uint8), [q_x[k]], group="st")
+        if lo:
+            c_k = act(T.yt[:, lo:lo + 128], bank(4 + k, 0, 128), ACT.Copy, [y_k], group="ya")
+        else:
+            dma("s", T.y[:, 128:C], T.yt[:, 128:C], [c_k], group="st")
+            c_k = cp(T.yt[:, lo:lo + 128], bank(4 + k, 0, 128), [y_k])
     for k in range(4):
         dma("ys"[k % 2], T.osc[4 * k:4 * k + 4, :], sn[32 * k:32 * k + 4, :], q_x, group="st")
-    dma("y", T.y[:, 0:128], T.yt[:, 0:128], [c_b], group="st")
+    dma("y", T.y[:, 0:128], T.yt[:, 0:128], [c_k], group="st")
     add(plan, "y", None, ["st"])
     add(plan, "g", None, [("sent", sends[0])])
     emit(plan, {"v": V, "s": A, "t": PE, "g": g, "y": g.sync}, T.sem)

@@ -5,23 +5,26 @@ ACT = ActivationFunctionType
 C, S, R = 384, 96, 2
 STEP = [2, 1]
 NW = C // 16
-S0, S1 = 14, 21
+E = 256
+BY_SCALAR = [(14, 21), (9, 17)]
+SUMS = [4, 8]
 NT = NW // 4
 BIG = 2.0 ** 40
 FAR = 2.0 ** 96
 KEY = 1024.0
 H = C // 2
+CUT = [0, H, C]
 X4, U8, BF, F32, U16, I32 = "float8_e4m3fn_x4", "uint8", "bfloat16", "float32", "uint16", "int32"
 WIDTH = [64 * a + 64 for a in range(NT)]
 START = [sum(WIDTH[a + 1:]) for a in range(NT)]
 WORDS = sum(WIDTH) + 64
 
 
-def weights(a):
-    return tuple(0.5 if S0 <= c < S1 else 1.0 for c in range(4 * a + 1, 4 * a + 5))
+def weights(r, a):
+    return tuple(0.5 if BY_SCALAR[r][0] <= c < BY_SCALAR[r][1] else 1.0 for c in range(4 * a + 1, 4 * a + 5))
 
 
-KINDS = sorted(set(weights(a) for a in range(NT)), reverse=True)
+KINDS = sorted(set(weights(r, a) for r in range(R) for a in range(NT)), reverse=True)
 
 SCRATCH = {
     "ps": ("psum", [128, 4096], F32),
@@ -39,7 +42,7 @@ SCRATCH = {
     "wide": ("sbuf", [128, 4 * C], BF), "jr": ("sbuf", [128, C], BF), "jc": ("sbuf", [128, C], BF),
     "iall": ("sbuf", [128, C + 8], F32),
     "ft": ("sbuf", [128, 4 * WORDS], BF), "qf": ("sbuf", [128, WORDS], X4), "sf": ("sbuf", [128, WORDS], U8),
-    "sg": ("sbuf", [128, S1 * C], BF), "sb": ("sbuf", [128, NW * H], BF),
+    "sg": ("sbuf", [128, NW * C], BF), "sb": ("sbuf", [128, NW * H], BF),
     "ef": ("sbuf", [128, C], F32), "yt": ("sbuf", [128, C], F32),
 }
 for _r in range(R + 1):
@@ -51,13 +54,13 @@ for _r in range(R):
                        ("dt", 4 * C, BF), ("z", 4 * C, BF), ("zs", 4 * C, BF), ("xs", 4 * C, BF),
                        ("qz", C, X4), ("sz", C, U8),
                        ("pm", C, F32), ("pw", C, F32), ("ne", C, BF), ("hc", C, BF), ("acc", 96, F32),
-                       ("oc_", C, BF), ("ec", C, BF), ("tab", 8 * C, BF), ("hs", 10 * C, BF),
+                       ("oc_", C, BF), ("ec", C, BF), ("tab", 9 * C, BF), ("hs", 10 * C, BF),
                        ("ka", 10 * C, F32), ("kb", 9 * C, F32), ("tl", 3 * C, F32), ("pc", C, BF),
                        ("off", 12 * NW, U16), ("oe", 4 * NW, U16)):
         SCRATCH["%s%d" % (_n, _r)] = ("sbuf", [128, _w], _d)
 
-POOLS = {"v": 48, "s": 36, "t": 12, "g": 10, "d": 24}
-SEMAPHORES = ["%s%d" % (k, i) for k in POOLS for i in range(POOLS[k])] + ["sent"] + \
+POOLS = {"v": 40, "s": 40, "t": 40, "g": 12}
+SEMAPHORES = ["%s%d" % (q, k) for q in POOLS for k in range(POOLS[q])] + ["d%d" % i for i in range(1, 8)] + ["sent"] + \
     ["%s%d" % (k, r) for k in ("aq", "ai", "ae") for r in range(R)]
 
 
@@ -77,44 +80,50 @@ def add(plan, queue, fn, deps=(), group=None, dma=False):
 
 def emit(plan, queues, sem):
     ops, groups = plan["ops"], plan["groups"]
-    known = {q: set() for q in queues}
-    past, waits, needed = {}, [], set()
-    for i, op in enumerate(ops):
+    known = {q: {} for q in queues}
+    past, waits, needed = [], [], set()
+    for op in ops:
+        want = {}
+        for d in op["deps"]:
+            if isinstance(d, tuple) or ops[groups[d][0] if d in groups else d]["dma"]:
+                want[d] = 1
+            else:
+                for m in groups.get(d, [d]):
+                    want[ops[m]["q"]] = max(want.get(ops[m]["q"], -1), m)
         mine, w = known[op["q"]], []
-        for d in reversed(op["deps"]):
-            if d in mine:
+        for key, at in sorted(want.items(), key=lambda kv: -kv[1]):
+            if mine.get(key, -1) >= at:
                 continue
-            w.append(d)
-            needed.add(d)
-            mine.add(d)
-            for m in (groups[d] if d in groups else [d]):
-                mine |= past.get(m, set())
+            w.append((key, at))
+            needed.add(at if key in queues else key)
+            mine[key] = at
+            for m in ([at] if key in queues else [] if isinstance(key, tuple) else groups.get(key, [key])):
+                for k2, at2 in past[m].items():
+                    mine[k2] = max(mine.get(k2, -1), at2)
         waits.append(w)
-        past[i] = set(mine)
-    last, count, where = {}, {}, {}
+        past.append(dict(mine))
+    count, last, where = {}, {}, {}
     for i, op in enumerate(ops):
         q = queues[op["q"]]
-        for d in waits[i]:
-            if isinstance(d, tuple):
-                q.wait_ge(sem[d[0]], d[1])
-            else:
-                q.wait_ge(sem[where[d]], where[d, "n"])
+        for key, at in waits[i]:
+            q.wait_ge(*((sem[key[0]], key[1]) if isinstance(key, tuple) else where[at if key in queues else key]))
         if op["fn"] is None:
             continue
         ins = op["fn"]()
-        key = op["group"] if op["group"] is not None else i
-        if key not in needed:
-            continue
-        step = 16 if op["dma"] else 1
-        if key not in where:
-            pool = "d" if op["dma"] else op["q"]
-            free = [n for n in ("%s%d" % (pool, k) for k in range(POOLS[pool])) if n not in last or last[n] in past[i]]
-            name = free[0]
-            last[name] = key
-            where[key] = name
-            count[name] = count.get(name, 0) + step * len(groups.get(key, [i]))
-            where[key, "n"] = count[name]
-        ins.then_inc(sem[where[key]], step)
+        if op["dma"]:
+            key = i if op["group"] is None else op["group"]
+            if key in needed:
+                if key not in where:
+                    count["d"] = count.get("d", 0) + 1
+                    where[key] = (sem["d%d" % count["d"]], 16 * len(groups.get(key, [i])))
+                ins.then_inc(where[key][0], 16)
+        elif i in needed:
+            pool = ["%s%d" % (op["q"], k) for k in range(POOLS[op["q"]])]
+            name = [n for n in pool if last.get(n, -1) <= past[i].get(op["q"], -1)][0]
+            last[name] = i
+            count[name] = count.get(name, 0) + 1
+            where[i] = (sem[name], count[name])
+            ins.then_inc(where[i][0], 1)
 
 
 def rank_program(g, core, T, topo):
@@ -174,10 +183,7 @@ def rank_program(g, core, T, topo):
         return gp(lambda: g.remote_dma(out, in_, T.sem[name], T.sem.sent, pid, rid, topo.mask(core, dst)), deps)
 
     ld_u = dma("s", T.ut[:], T.u[:])
-    ld_x = [dma("y", T.x0[:, 0:2 * C], T.x[:, 0:2 * C]), dma("y", T.x0[:, 2 * C:4 * C], T.x[:, 2 * C:4 * C])]
-    ld_w = dma("y", T.qw[:].bitcast(dt.uint8), T.wc[:], ld_x, group="ldw")
-    dma("y", T.sw[:], T.ws[:], group="ldw")
-    ld_v = dma("y", T.vt[:], T.v[:])
+    ld_x = [dma("y", T.x0[:, 0:4 * E], T.x[:, 0:4 * E]), dma("y", T.x0[:, 4 * E:4 * C], T.x[:, 4 * E:4 * C])]
 
     fl_ok = {"allow_small_or_imprecise_dtypes": True}
     ip = gp(lambda: g.iota(T.ci[:, 0:2], [[0, 2]], 0, 1))
@@ -185,7 +191,7 @@ def rank_program(g, core, T, topo):
     iu = gp(lambda: g.iota(T.ci[:, 24:56], [[1, 8], [0, 4]], 0, 0), group="iu")
     it = gp(lambda: g.iota(T.cf[:, 0:NW + 1], [[1, NW + 1]], -1, 0, **fl_ok))
     c_jr = gp(lambda: g.iota(T.jr[:], [[0, NW], [1, 16]], 0, 0, **fl_ok))
-    one = gp(lambda: g.iota(T.ones[:], [[0, 528]], 1, 0, **fl_ok))
+    c_jc = gp(lambda: g.iota(T.jc[:], [[1, C]], -H, 0, **fl_ok))
 
     def col(k):
         return T.cf[:, k:k + 1]
@@ -196,43 +202,36 @@ def rank_program(g, core, T, topo):
     def wide(k):
         return T.wide[:, C * k:C * k + C]
 
-    def clear(a):
+    blank = v(lambda: V.memset(T.ft[:, 4 * START[0]:4 * WORDS], 0.0))
+    for a in range(1, NT):
         end = START[a] + WIDTH[a]
-        return v(lambda: V.memset(T.ft[:, 4 * (end - 48):4 * (end if a else WORDS)], 0.0), group="zero")
+        zero = dma("y", T.ft[:, 4 * (end - 48):4 * end], T.ft[:, 4 * (WORDS - 48):4 * WORDS], [blank, ld_x[0]], group="zero")
+    ld_w = dma("y", T.qw[:].bitcast(dt.uint8), T.wc[:], ld_x, group="ldw")
+    dma("y", T.sw[:], T.ws[:], group="ldw")
+    ld_v = dma("y", T.vt[:], T.v[:])
 
     less1, t16, t24 = T.cf[:, 0:16], T.cf[:, 1:17], T.cf[:, 1:NW + 1]
     qcol, gcol, rcol, hcol = col(32), col(33), col(34), col(35)
     sc16, scm, sc4, add4, big16, base = col(36), col(37), col(38), col(39), col(40), col(41)
-    clear(0)
     ts(T.ci[:, 4:5], T.ci[:, 0:1], 15, ALU.bitwise_and, deps=[ip], group="pi")
     pi = ts(T.ci[:, 5:6], T.ci[:, 0:1], 4, ALU.logical_shift_right, deps=[ip], group="pi")
-    clear(1)
     pf = cp(T.cf[:, 32:34], T.ci[:, 4:6], [pi])
     uo = cp(T.cu[:, 48:88], T.ci[:, 16:56], [iu])
     k_grp = ts(small(0), t16, gcol, ALU.is_equal, deps=[it, pf])
-    for a in range(2, NT):
-        zero = clear(a)
+    late = {}
     q_u = quant(T.qu[:], T.su[:], T.ut[:], [ld_u])
+    padded = quant(T.qf[:, WORDS - 128:WORDS], T.sf[:, WORDS - 128:WORDS], T.ft[:, 4 * (WORDS - 128):4 * WORDS], [blank])
     cp(T.qur[:].bitcast(dt.uint32), T.qu[:].bitcast(dt.uint32).indirect(T.cu[:, 48:56]), [uo, q_u], group="ur")
-    q_ur = cp(T.sur[:], T.su[:].indirect(T.cu[:, 48:56]), [uo, q_u], group="ur")
-    q_x = [quant(T.qx0[:, 0:H], T.sx0[:, 0:H], T.x0[:, 0:2 * C], [ld_x[0]])]
-    w_own = ts(wide(0), T.jr[:], qcol, ALU.not_equal, FAR, ALU.mult, [pf, c_jr])
-    q_x.append(quant(T.qx0[:, H:C], T.sx0[:, H:C], T.x0[:, 2 * C:4 * C], [ld_x[1]]))
-    w_new = ts(wide(1), T.jr[:], 0.0, ALU.is_equal, FAR, ALU.mult, [c_jr])
-    k_a16 = ts(small(2), t16, qcol, ALU.is_gt, deps=[it, pf])
-    k_c16 = ts(small(8), less1, qcol, ALU.is_equal, BIG, ALU.mult, [it, pf])
-    c_bd = act(T.bw[:, 0:512], small(0).indirect(T.cu[:, 56:88]), ACT.Copy, [uo, k_grp])
+    c_bw = [act(T.bw[:, 0:512], small(0).indirect(T.cu[:, 56:88]), ACT.Copy, [uo, k_grp])]
+    q_ur = act(T.sur[:], T.su[:].indirect(T.cu[:, 48:56]), ACT.Copy, [uo, q_u], group="ur")
     for k, w in list(enumerate(KINDS))[1:]:
         for t, step in ([(0, 1)] if len(set(w)) == 1 else [(t, 4) for t in range(4)]):
-            c_bw = act(T.bw[:, 512 * k + t:512 * k + 512:step], T.bw[:, t:512:step], ACT.Copy, [c_bd], group="bw", scale=w[t])
-    x_made = list(ld_x)
-    psum_free = []
-    late = {}
-    late["qo"] = ts(T.cu[:, 0:NW], t24, 0.0, ALU.mult, qcol, ALU.add, [it, pf])
-    late["sc"] = ts(sc16, qcol, 15.0, ALU.is_equal, 1.0 / BIG, ALU.max, [pf])
-    late["up"] = ts(col(42), qcol, 15.0, ALU.is_lt, BIG, ALU.mult, [pf])
-    late["h16"] = tt(small(3), small(8), small(2), ALU.max, [k_a16, k_c16])
-    late["bd"] = quant(T.qb[:], T.sq[:], T.bw[:], [c_bw])
+            made = act(T.bw[:, 512 * k + t:512 * k + 512:step], T.bw[:, t:512:step], ACT.Copy, [c_bw[0]], scale=w[t])
+        c_bw.append(made)
+
+    def adder(k):
+        late["bd", k] = quant(T.qb[:, 128 * k:128 * k + 128], T.sq[:, 128 * k:128 * k + 128],
+                              T.bw[:, 512 * k:512 * k + 512], [c_bw[k]])
 
     def unpacker(b):
         return lambda: late.update(qe=quant(T.qe[:, 128 * b:128 * b + 128], T.se[:, 128 * b:128 * b + 128],
@@ -245,16 +244,193 @@ def rank_program(g, core, T, topo):
         [lambda: late.update(a4=ts(small(5), t16, hcol, ALU.is_gt, deps=[it, late["pg"]])),
          lambda: late.update(c4=ts(small(9), less1, hcol, ALU.is_equal, BIG, ALU.mult, [it, late["pg"]]))],
         [lambda: late.update(ro=ts(T.cu[:, NW:2 * NW], t24, 0.0, ALU.mult, rcol, ALU.add, [it, late["pg"]])),
-         lambda: late.update(h4=tt(small(4), small(9), small(5), ALU.max, [late["a4"], late["c4"]]))],
+         lambda: late.update(s4=ts(col(43), hcol, 3.0, ALU.is_equal, 1.0 / BIG, ALU.max, [late["pg"]]))],
         [unpacker(0)], [unpacker(1)], [unpacker(2)], [unpacker(3)],
-        [lambda: late.update(s4=ts(col(43), hcol, 3.0, ALU.is_equal, 1.0 / BIG, ALU.max, [late["pg"]]))],
         [lambda: late.update(qv=quant(T.qv[:], T.sv[:], T.vt[:], [ld_v]))],
     ]
 
     def gap():
-        if gaps:
-            for f in gaps.pop(0):
-                f()
+        for make in (gaps.pop(0) if gaps else []):
+            make()
+
+    def places(r, state):
+        mate = T.cores[rank ^ STEP[r]]
+        qx, sx, pm, pw, nb, acc, hc, off = [T["%s%d" % (n, r)] for n in ("qx", "sx", "pm", "pw", "ne", "acc", "hc", "off")]
+        ft, sb, sg = T.ft, T.sb, T.sg
+        (S0, S1), K, turned = BY_SCALAR[r], SUMS[r], r > 0
+        rows, within, signs, order = {}, {}, [], []
+
+        def score(lo, hi):
+            return bank(4, lo, hi) if hi <= E else bank(0, lo - E * turned, hi - E * turned)
+
+        def own(lo, hi, made):
+            return tt(pm[:, lo:hi], score(lo, hi), T.wide[:, lo:hi], ALU.add, [w_own, made])
+
+        def hold(lo, hi, m):
+            return scan(pw[:, lo:hi], T.wide[:, C + lo:C + hi], pm[:, lo:hi], 0.0, ALU.add, ALU.min, [w_new, m])
+
+        def flags(c, lo, hi, step=4, first=0):
+            at = 4 * START[(c - 1) // 4] + (c - 1) % 4
+            return ft[:, at + 4 * lo + first:at + 4 * hi - 3:step]
+
+        def mine(c):
+            return pw[:, 16 * c + 15:16 * c + 16]
+
+        def by_scalar(cs, deps):
+            for c in cs:
+                if c:
+                    signs.append((c, act(sg[:, C * c:C * c + 16 * c], bank(5 if 16 * c <= E else 1, 0, 16 * c), ACT.Sign,
+                                         deps, bias=mine(c), scale=-1.0)))
+                if len(signs) == 2 or not c:
+                    d, sign = signs.pop(0)
+                    rows[d] = act(flags(d, 0, 16 * d), sg[:, C * d:C * d + 16 * d], ACT.Sign, [zero, sign], scale=-1.0,
+                                  bias=-0.5 if turned and 16 * d >= E else 0.5, accum_out=acc[:, d:d + 1])
+
+        def compare(cs, held):
+            for c in cs:
+                if 16 * c < E or not turned:
+                    rows[c] = ts(flags(c, 0, 16 * c), score(0, 16 * c), mine(c), ALU.is_ge, 0.5, ALU.subtract, [zero, held])
+                else:
+                    ts(flags(c, 0, E), score(0, E), mine(c), ALU.is_gt, 0.5, ALU.subtract, [zero, held])
+                    rows[c] = ts(flags(c, E, 16 * c), score(E, 16 * c), mine(c), ALU.is_ge, 0.5, ALU.subtract)
+
+        def sixteens(lo, hi, held):
+            rows[NW] = tt(flags(NW, lo, hi), score(lo, hi), pw[:, lo:hi], ALU.is_gt, [zero, held])
+            return rows[NW]
+
+        def runs(lo, hi, made):
+            within[lo] = scan(nb[:, lo:hi], T.wide[:, lo:hi], flags(NW, lo, hi), 0.0, ALU.min, ALU.add, [made])
+
+        def add_up(cs):
+            for c in cs:
+                scan(sb[:, H * c + H - 8 * c:H * c + H], flags(c, 0, 16 * c, 8), flags(c, 0, 16 * c, 8, 4),
+                     nb[:, 16 * c + 15:16 * c + 16], ALU.add, ALU.add, [within[E * (16 * c >= E)], rows[c]], group="cnt%d" % r)
+
+        def add_up_short():
+            for c in range(K, 0, -1):
+                rows[c] = act(sg[:, C * c:C * c + 16 * c], flags(c, 0, 16 * c), ACT.Copy, [rows[c]], scale=2.0,
+                              accum_out=acc[:, c:c + 1])
+
+        def pack(tiles):
+            lo, hi = START[tiles[0]], START[tiles[-1]] + WIDTH[tiles[-1]]
+            done = quant(T.qf[:, lo:hi], T.sf[:, lo:hi], ft[:, 4 * lo:4 * hi],
+                         [padded] + [rows[c] for a in tiles for c in range(4 * a + 1, 4 * a + 5)])
+            for a in tiles:
+                k, n = 128 * KINDS.index(weights(r, a)), max(128, WIDTH[a])
+                order.append(a)
+                mm(6, n, T.qb[:, k:k + 128], T.sq[:, k:k + 128], T.qf[:, START[a]:START[a] + n],
+                   T.sf[:, START[a]:START[a] + n], [late["bd", k // 128], done],
+                   group="down%d" % r, start=len(order) == 1, stop=len(order) == NT)
+
+        def send():
+            remote(mate, T["ls%d" % r][:], sx[:], "aq%d" % r, state["early"] + state["late"])
+
+        at = (C - E) * turned
+        p_v = mm(4, E, T.qur[:], T.sur[:], qx[:, at:at + E], sx[:, at:at + E], [q_ur] + state["banks_early"] + state["early"])
+        p_s = mm(5, E, T.qur[:], T.sur[:], qx[:, at:at + E], sx[:, at:at + E])
+        none = act(acc[:, 0:1], col(1), ACT.Copy, [it], scale=0.0)
+        yield
+        if not turned:
+            yield
+            p_l = mm(0, C, T.qur[:], T.sur[:], qx[:], sx[:], state["late"])
+            p_a = mm(1, C, T.qur[:], T.sur[:], qx[:], sx[:])
+            send()
+            made = [own(16 * S0, E, p_v), own(0, 16 * S0, p_v)]
+            pw_s, pw_e = hold(16 * S0, E, made[0]), hold(0, 16 * S0, made[1])
+            by_scalar([15, 14], [p_s, pw_s])
+            m_l = own(E, C, p_l)
+            f_e = sixteens(0, E, pw_e)
+            pw_l = hold(E, C, m_l)
+            by_scalar([20, 19, 18, 17, 16, None], [p_a, pw_l])
+            next(state["soon"])
+            runs(0, E, f_e)
+            compare([23, 22, 21], pw_l)
+            f_l = sixteens(E, C, pw_l)
+            compare([13], pw_e)
+            runs(E, C, f_l)
+            pack([5])
+            compare(range(8, 0, -1), pw_e)
+            next(state["soon"])
+            pack([1, 0])
+            add_up_short()
+            compare([12, 11, 10], pw_e)
+            pack([4])
+            compare([9], pw_e)
+            pack([3])
+            pack([2])
+            last = [23, 22, 21] + list(range(S0 - 1, K, -1))
+        else:
+            made = [own(16 * 13, E, p_v), own(0, 16 * 13, p_v)]
+            yield
+            p_l = mm(0, C - E, T.qur[:], T.sur[:], qx[:, 0:C - E], sx[:, 0:C - E], state["banks_late"] + state["late"])
+            send()
+            pw_s, pw_e = hold(16 * 13, E, made[0]), hold(0, 16 * 13, made[1])
+            yield
+            by_scalar([15, 14, 13], [p_s, pw_s])
+            f_e = sixteens(0, E, pw_e)
+            m_l = own(E, C, p_l)
+            compare(range(S0 - 1, 3, -1), pw_e)
+            pw_l = hold(E, C, m_l)
+            by_scalar([16] + list(range(12, S0 - 1, -1)) + [None], [pw_l])
+            compare([3, 2, 1], pw_e)
+            runs(0, E, f_e)
+            compare([23, 22, 21], pw_l)
+            f_l = sixteens(E, C, pw_l)
+            compare([20], pw_l)
+            runs(E, C, f_l)
+            pack([5])
+            pack([1, 0])
+            pack([3])
+            compare([19, 18, 17], pw_l)
+            pack([2])
+            pack([4])
+            add_up_short()
+            last = list(range(NW - 1, S1 - 1, -1)) + list(range(S0 - 1, K, -1))
+        yield
+        spans = [(0, S1)] if K + 1 == S0 else [(S0, S1), (0, K + 1)]
+        rows[0] = none
+        add_up(last[:-3])
+        by_s = [ts(acc[:, 64 + lo:64 + hi], acc[:, lo:hi], 0.5, ALU.mult, deps=[rows[c] for c in range(lo, hi)])
+                for lo, hi in spans]
+        add_up(last[-3:])
+        for k, (lo, hi) in enumerate(spans):
+            tt(sb[:, H * lo + H - 1:H * hi:H], acc[:, 64 + lo:64 + hi], nb[:, 16 * lo + 15:16 * hi:16], ALU.add,
+               list(within.values()) + [by_s[k]], group="cnt%d" % r)
+        h_c = [scan(hc[:, 0:E], T.wide[:, 2 * C:2 * C + E], bank(6, 0, E), 0.0, ALU.mult, ALU.add, [late["w16"], "down%d" % r])]
+        along = ts(acc[:, 32:32 + NW], sb[:, H - 1:H * NW:H], big16, ALU.mult, deps=[late["big"], "cnt%d" % r])
+        h_c.append(scan(hc[:, E:C], T.wide[:, 2 * C + E:3 * C], bank(6, E, C), 0.0, ALU.mult, ALU.add))
+        both = [tt(acc[:, (lo + at) % C // 16:(lo + at) % C // 16 + (hi - lo) // 16], acc[:, 32 + lo // 16:32 + hi // 16],
+                   hc[:, lo + 15:hi:16], ALU.subtract, [along, h_c[k]]) for k, (lo, hi) in enumerate(((0, E), (E, C)))]
+        state["places"] = ts(off[:, 0:NW], acc[:, 0:NW], sc16, ALU.mult, base, ALU.add, [late["sc"], late["base"]] + both)
+        remote(mate, T["li%d" % r][:], off[:, 0:NW], "ai%d" % r, [state["places"]])
+        remote(mate, T["lq%d" % r][:].bitcast(dt.uint8), qx[:].bitcast(dt.uint8), "aq%d" % r, [])
+        yield
+
+    state = {"banks_early": [], "banks_late": [], "late": []}
+    steps = places(0, state)
+    state["early"] = [quant(T.qx0[:, 0:E], T.sx0[:, 0:E], T.x0[:, 0:4 * E], [ld_x[0]])]
+    next(steps)
+    w_own = ts(wide(0), T.jr[:], qcol, ALU.not_equal, FAR, ALU.mult, [pf, c_jr])
+    q_l = quant(T.qx0[:, E:C], T.sx0[:, E:C], T.x0[:, 4 * E:4 * C], [ld_x[1]])
+    w_new = ts(wide(1), T.jr[:], 0.0, ALU.is_equal, FAR, ALU.mult, [c_jr])
+    adder(0)
+    k_a16 = ts(small(2), t16, qcol, ALU.is_gt, deps=[it, pf])
+    k_c16 = ts(small(8), less1, qcol, ALU.is_equal, BIG, ALU.mult, [it, pf])
+    next(steps)
+    state["late"] = [q_l]
+
+    def soon():
+        late["qo"] = ts(T.cu[:, 0:NW], t24, 0.0, ALU.mult, qcol, ALU.add, [it, pf])
+        late["h16"] = tt(small(3), small(8), small(2), ALU.max, [k_a16, k_c16])
+        yield
+        late["sc"] = ts(sc16, qcol, 15.0, ALU.is_equal, 1.0 / BIG, ALU.max, [pf])
+        late["up"] = ts(col(42), qcol, 15.0, ALU.is_lt, BIG, ALU.mult, [pf])
+        for k in range(1, len(KINDS)):
+            adder(k)
+        yield
+
+    state["soon"] = soon()
+    x_made = list(ld_x)
 
     for r in range(R):
         mate = T.cores[rank ^ STEP[r]]
@@ -272,151 +448,97 @@ def rank_program(g, core, T, topo):
         def part(buf, k):
             return buf[:, C * k:C * k + C]
 
-        p_v = mm(0, C, T.qur[:], T.sur[:], qx[:], sx[:], [q_ur] + psum_free + q_x)
-        p_s = mm(1, C, T.qur[:], T.sur[:], qx[:], sx[:], [q_ur] + psum_free + q_x)
-        remote(mate, B("lq")[:].bitcast(dt.uint8), qx[:].bitcast(dt.uint8), "aq%d" % r, q_x)
-        remote(mate, B("ls")[:], sx[:], "aq%d" % r, q_x)
+        next(steps)
         if r == 0:
-            c_jc = gp(lambda: g.iota(T.jc[:], [[1, C]], -H, 0, **fl_ok))
+            late["w16"] = act(wide(2), small(3).indirect(T.cu[:, 0:NW]), ACT.Copy, [late["qo"], late["h16"]])
+            late["big"] = act(big16, col(42), ACT.Identity, [late["up"]], bias=1.0)
+            late["base"] = act(base, qcol, ACT.Identity, [pf], bias=H - 8.0)
+        fill_o = act(B("oc_")[:], T.jr[:], ACT.Copy, [c_jr], scale=0.0)
+        next(steps)
+        if r == 0:
+            one = gp(lambda: g.iota(T.ones[:], [[0, 528]], 1, 0, **fl_ok))
             late["et"] = gp(lambda: g.affine_select(T.et[:], T.ones[:], [[-1, 528]], ALU.is_equal, 0.0, 3, 4), [one])
             c_i = gp(lambda: g.iota(T.iall[:], [[int(KEY), C + 8]], -int(KEY), 0, **fl_ok))
-
-        pm, pw, nb, acc, ft, sb, sg = B("pm"), B("pw"), B("ne"), B("acc"), T.ft, T.sb, T.sg
-
-        def own(lo, hi):
-            return tt(pm[:, lo:hi], bank(0, lo, hi), T.wide[:, lo:hi], ALU.add, [w_own, p_v])
-
-        def hold(lo, hi, m):
-            return scan(pw[:, lo:hi], T.wide[:, C + lo:C + hi], pm[:, lo:hi], 0.0, ALU.add, ALU.min, [w_new, m])
-
-        def flags(c, n, step=4, first=0):
-            at = 4 * START[(c - 1) // 4] + (c - 1) % 4
-            return ft[:, at + first:at + 4 * n - 3:step]
-
-        def mine(c):
-            return pw[:, 16 * c + 15:16 * c + 16]
-
-        m_s, m_hi, m_lo = own(16 * S0, 16 * S1), own(16 * S1, C), own(0, 16 * S0)
-        pw_s, pw_hi, pw_lo = hold(16 * S0, 16 * S1, m_s), hold(16 * S1, C, m_hi), hold(0, 16 * S0, m_lo)
-        rows, signs = {}, []
-        for c in list(range(S1 - 1, S0 - 1, -1)) + [None]:
-            if c:
-                signs.append((c, act(sg[:, C * c:C * c + 16 * c], bank(1, 0, 16 * c), ACT.Sign,
-                                     [p_s, pw_s], bias=mine(c), scale=-1.0)))
-            if len(signs) == 2 or not c:
-                d, sign = signs.pop(0)
-                rows[d] = act(flags(d, 16 * d), sg[:, C * d:C * d + 16 * d], ACT.Sign,
-                              [zero, sign], bias=0.5, scale=-1.0, accum_out=acc[:, d:d + 1])
-
-        def mine_v(a):
-            return [c for c in range(min(4 * a + 4, NW - 1), 4 * a, -1) if not S0 <= c < S1]
-
-        def compare(a, held):
-            for c in mine_v(a):
-                rows[c] = ts(flags(c, 16 * c), bank(0, 0, 16 * c), mine(c), ALU.is_ge, 0.5, ALU.subtract, [zero, held],
-                             group="cmp%d_%d" % (r, a))
-
-        def add_up(cs):
-            for c in cs:
-                scan(sb[:, H * c + H - 8 * c:H * c + H], flags(c, 16 * c, 8), flags(c, 16 * c, 8, 4),
-                     nb[:, 16 * c + 15:16 * c + 16], ALU.add, ALU.add, [within, rows[c]], group="cnt%d" % r)
-
-        order = []
-
-        def pack(tiles):
-            lo, hi = START[tiles[0]], START[tiles[-1]] + max(128, WIDTH[tiles[-1]])
-            done = quant(T.qf[:, lo:hi], T.sf[:, lo:hi], ft[:, 4 * lo:4 * hi],
-                         [rows[c] for a in tiles for c in range(4 * a + 1, 4 * a + 5)])
-            for a in tiles:
-                k, n = 128 * KINDS.index(weights(a)), max(128, WIDTH[a])
-                order.append(a)
-                mm(6, n, T.qb[:, k:k + 128], T.sq[:, k:k + 128], T.qf[:, START[a]:START[a] + n],
-                   T.sf[:, START[a]:START[a] + n], [late["bd"]] + psum_free + [done],
-                   group="down%d" % r, start=len(order) == 1, stop=len(order) == NT)
-
-        compare(5, pw_hi)
-        rows[NW] = tt(flags(NW, C), bank(0, 0, C), pw[:], ALU.is_gt, [pw_s, pw_hi, pw_lo])
-        if r == 0:
-            w_h16 = act(wide(2), small(3).indirect(T.cu[:, 0:NW]), ACT.Copy, [late["qo"], late["h16"]])
-            k_big = act(big16, col(42), ACT.Identity, [late["up"]], bias=1.0)
-            k_base = act(base, qcol, ACT.Identity, [pf], bias=H - 8.0)
-            k_sc = late["sc"]
-        fill_o = act(B("oc_")[:], T.jr[:], ACT.Copy, [c_jr], scale=0.0)
-        compare(3, pw_lo)
-        compare(2, pw_lo)
-        within = scan(nb[:], wide(0), flags(NW, C), 0.0, ALU.min, ALU.add, [rows[NW]])
-        pack([5])
-        cp(sb[:, H - 1:H], nb[:, 15:16], [within], group="cnt%d" % r)
-        compare(1, pw_lo)
-        compare(0, pw_lo)
-        pack([4])
-        add_up(mine_v(5))
-        pack([2, 1, 0])
-        add_up(mine_v(3) + mine_v(2))
-        pack([3])
-        by_s = ts(acc[:, 64 + S0:64 + S1], acc[:, S0:S1], 0.5, ALU.mult, deps=[rows[c] for c in range(S0, S1)])
-        add_up(mine_v(1))
-        tt(sb[:, H * S0 + H - 1:H * S1:H], acc[:, 64 + S0:64 + S1], nb[:, 16 * S0 + 15:16 * S1:16], ALU.add, [within, by_s],
-           group="cnt%d" % r)
-        add_up(mine_v(0))
-        h_c = scan(B("hc")[:], wide(2), bank(6, 0, C), 0.0, ALU.mult, ALU.add, [w_h16, "down%d" % r])
-        along = ts(acc[:, 32:32 + NW], sb[:, H - 1:H * NW:H], big16, ALU.mult, deps=[k_big, "cnt%d" % r])
-        both = tt(acc[:, 0:NW], acc[:, 32:32 + NW], B("hc")[:, 15:C:16], ALU.subtract, [h_c, along])
-        i_w = ts(offs(0), acc[:, 0:NW], sc16, ALU.mult, base, ALU.add, [k_sc, k_base, both])
-        remote(mate, B("li")[:], offs(0), "ai%d" % r, [i_w])
-        o_c = cp(B("oc_")[:].indirect(offs(0)), T.jc[:], [c_jc, fill_o, i_w])
+        o_c = cp(B("oc_")[:].indirect(offs(0)), T.jc[:], [c_jc, fill_o, state["places"]])
         fill_e = act(B("ec")[:], T.jr[:], ACT.Copy, scale=0.0)
 
         tab, hs, ka, kb = B("tab"), B("hs"), B("ka"), B("kb")
         came = ("ai%d" % r, ne)
 
-        w_half = T.wide[:, 2 * C:2 * C + H]
-
         def half(buf, k, h):
-            return buf[:, C * k + H * h:C * k + H * h + H]
+            return buf[:, C * k + CUT[h]:C * k + CUT[h + 1]]
 
         def list_half(tile, k, h):
-            return tile[:, NW * k + NW // 2 * h:NW * k + NW // 2 * (h + 1)]
+            return tile[:, NW * k + CUT[h] // 16:NW * k + CUT[h + 1] // 16]
 
         def wrap(src, k, via, to, made):
-            lifted = [scan(half(hs, via, h), w_half, half(src, k, h), 0.0, ALU.mult, ALU.add, [made[h]]) for h in range(2)]
-            return [ts(list_half(off, to, h), hs[:, C * via + H * h + 15:C * via + H * h + H:16], sc16, ALU.mult,
+            lifted = [scan(half(hs, via, h), half(T.wide, 2, h), half(src, k, h), 0.0, ALU.mult, ALU.add, [made[h]])
+                      for h in range(2)]
+            return [ts(list_half(off, to, h), hs[:, C * via + CUT[h] + 15:C * via + CUT[h + 1]:16], sc16, ALU.mult,
                        float(H), ALU.add, [lifted[h]]) for h in range(2)]
 
-        a_k = [ts(half(ka, 0, h), B("oc_")[:].indirect(list_half(B("li"), 0, h)), KEY, ALU.mult, KEY * H + C, ALU.add,
-                  [came, o_c]) for h in range(2)]
-        t_k, o_k = [came, o_c], [None, None]
+        def third(buf, k, h):
+            return buf[:, C * k + 128 * h:C * k + 128 * h + 128]
+
+        def list_third(tile, k, h):
+            return tile[:, NW * k + 8 * h:NW * k + 8 * h + 8]
+
+        def key(k, h, deps):
+            if k == 0:
+                return ts(third(ka, 0, h), B("oc_")[:].indirect(list_third(B("li"), 0, h)), KEY, ALU.mult, KEY * H + C, ALU.add,
+                          [came, o_c])
+            return tt(third(ka, k, h), part(ka, k - 1).indirect(list_third(off, k, h)), third(kb, k - 1, h), ALU.min, deps)
+
+        def lift(k, h):
+            return scan(third(hs, k, h), third(T.wide, 2, h), third(tab, k, h), 0.0, ALU.mult, ALU.add, [t_k[h]])
+
+        def listed_as(k, h, lifted):
+            return ts(list_third(off, k + 1, h), hs[:, C * k + 128 * h + 15:C * k + 128 * h + 128:16], sc16, ALU.mult,
+                      float(H), ALU.add, [lifted])
+
+        a_k = [key(0, 0, []), key(0, 1, [])]
+        t_k, o_k, last = [came, o_c], [None] * 3, []
         for k in range(8):
             lst = off if k else B("li")
-            t_k = [act(half(tab, k, h), (part(tab, k - 1) if k else B("oc_")[:]).indirect(list_half(lst, k, h)), ACT.Copy,
-                       t_k + [o_k[h]]) for h in range(2)]
-            b_k = [act(half(kb, k, h), half(ka, k, h), ACT.Identity, [a_k[h]], bias=-float(2 ** k)) for h in range(2)]
-            o_k = wrap(tab, k, k, k + 1, t_k)
-            a_k = [tt(half(ka, k + 1, h), part(ka, k).indirect(list_half(off, k + 1, h)), half(kb, k, h), ALU.min,
-                      a_k + [o_k[h], b_k[h]]) for h in range(2)]
+            t_k = [act(third(tab, k, h), (part(tab, k - 1) if k else B("oc_")[:]).indirect(list_third(lst, k, h)), ACT.Copy,
+                       t_k + [o_k[h]]) for h in range(3)]
+            s_0 = lift(k, 0)
+            a_k.append(key(k, 2, last))
+            b_k = [act(third(kb, k, h), third(ka, k, h), ACT.Identity, [a_k[h]], bias=-float(2 ** k)) for h in range(3)]
+            s_1 = lift(k, 1)
+            o_k = [listed_as(k, 0, s_0)]
             gap()
+            s_2 = lift(k, 2)
+            o_k.append(listed_as(k, 1, s_1))
+            a_n = [key(k + 1, 0, a_k + [o_k[0], b_k[0]])]
+            o_k.append(listed_as(k, 2, s_2))
+            a_n.append(key(k + 1, 1, [o_k[1], b_k[1]]))
+            a_k, last = a_n, [o_k[2], b_k[2]]
         b_last = act(part(kb, 8), part(ka, 7), ACT.Identity, b_k, bias=-256.0)
-        gap()
+        a_k.append(key(8, 2, last))
         if r == 0:
-            w_h4 = act(wide(3), small(4).indirect(T.cu[:, NW:2 * NW]), ACT.Copy, [late["ro"], late["h4"]])
-            k_scm = act(scm, sc16, ACT.Copy, [k_sc], scale=1.0 / KEY)
-            k_sc4 = act(sc4, col(43), ACT.Copy, [late["s4"]], scale=4.0)
-            k_add4 = act(add4, rcol, ACT.Identity, [late["pg"]], bias=4.0 * H)
-        for b in range(4):
-            d_mm = mm(2 + b, C, T.qe[:, 128 * b:128 * b + 128], T.se[:, 128 * b:128 * b + 128], B("lq")[:], B("ls")[:],
-                      [late["qe"], ("aq%d" % r, 2 * ne)] + psum_free)
-            d_cp = act(B("dt")[:, b:4 * C:4], bank(2 + b, 0, C), ACT.Copy, [d_mm], group="dcp%d" % r)
-        tl, pc, oe = B("tl"), B("pc"), B("oe")
+            late["h4"] = tt(small(4), small(9), small(5), ALU.max, [late["a4"], late["c4"]])
         a_k = [tt(half(ka, 9, h), part(ka, 8).indirect(list_half(off, 8, h)), half(kb, 8, h), ALU.min, [b_last] + a_k)
                for h in range(2)]
+        if r == 0:
+            w_h4 = act(wide(3), small(4).indirect(T.cu[:, NW:2 * NW]), ACT.Copy, [late["ro"], late["h4"]])
+            k_scm = act(scm, sc16, ACT.Copy, scale=1.0 / KEY)
+            k_sc4 = act(sc4, col(43), ACT.Copy, [late["s4"]], scale=4.0)
+            k_add4 = act(add4, rcol, ACT.Identity, [late["pg"]], bias=4.0 * H)
+        for b, at in enumerate((1, 2, 3, 7)):
+            d_mm = mm(at, C, T.qe[:, 128 * b:128 * b + 128], T.se[:, 128 * b:128 * b + 128], B("lq")[:], B("ls")[:],
+                      [late["qe"], ("aq%d" % r, 2 * ne)] + state["banks_early"] + state["banks_late"])
+            d_cp = act(B("dt")[:, b:4 * C:4], bank(at, 0, C), ACT.Copy, [d_mm], group="dcp%d" % r)
+        tl, pc, oe = B("tl"), B("pc"), B("oe")
         top, h_m = [], []
         for h in range(2):
-            top.append(scan(half(tl, 1, h), half(ka, 9, h), T.iall[:, 1 + H * h:1 + H * h + H], -1.0e6, ALU.max, ALU.max,
+            top.append(scan(half(tl, 1, h), half(ka, 9, h), T.iall[:, 1 + CUT[h]:1 + CUT[h + 1]], -1.0e6, ALU.max, ALU.max,
                             [c_i, a_k[h]]))
-            h_m.append(scan(half(tl, 0, h), w_half, half(ka, 9, h), 0.0, ALU.mult, ALU.add, [a_k[h]]))
+            h_m.append(scan(half(tl, 0, h), half(T.wide, 2, h), half(ka, 9, h), 0.0, ALU.mult, ALU.add, [a_k[h]]))
+        m_w = [ts(list_half(off, 9, 0), tl[:, 15:CUT[1]:16], scm, ALU.mult, deps=[k_scm, h_m[0]])]
         ends = scan(part(tl, 2), part(tl, 1), T.iall[:, 0:C], -KEY - H, ALU.add, ALU.subtract, top)
-        m_w = ts(offs(9), tl[:, 15:C:16], scm, ALU.mult, deps=[k_scm] + h_m)
-        pos = [tt(half(pc, 0, h), part(tl, 2).indirect(list_half(off, 9, h)), half(ka, 9, h), ALU.subtract, [ends, m_w])
+        m_w.append(ts(list_half(off, 9, 1), tl[:, CUT[1] + 15:C:16], scm, ALU.mult, deps=[h_m[1]]))
+        pos = [tt(half(pc, 0, h), part(tl, 2).indirect(list_half(off, 9, h)), half(ka, 9, h), ALU.subtract, [m_w[h], ends])
                for h in range(2)]
         o_p = wrap(pc, 0, 8, 10, pos)
         e_c = cp(B("ec")[:].indirect(offs(10)), T.jc[:], [fill_e] + o_p)
@@ -451,36 +573,51 @@ def rank_program(g, core, T, topo):
                                       zs[:, 4 * lo + b:4 * lo + 512:4], ALU.add, deps + [made[b]])]
             return [free[first + b][0] for b in bs]
 
-        def state(lo, deps):
+        def packed(lo, deps):
             return quant(qn[:, lo:lo + 128], sn[:, lo:lo + 128], Xn[:, 4 * lo:4 * lo + 512], deps)
 
         listed = x_made + [o_e[1]]
-        g_b = [pick("s", 96, 128, X, oe, x_made + [o_e[0]])]
         g_1 = [pick("v", 128, 192, X, oe, listed), pick("s", 192, 256, X, oe, listed)]
-        g_2 = [pick("v", 256, 320, X, oe, listed), pick("s", 320, 384, X, oe, listed)]
-        if r == R - 1:
-            e_f = act(T.ef[:], B("ec")[:], ACT.Identity, [e_c], bias=float(H))
-            dma("y", T.el[:], T.ef[0:128:16, :], [e_f], group="st")
+        g_2 = [pick("v", 256, 304, X, oe, listed), pick("s", 304, 384, X, oe, listed)]
+        g_b = [pick("s", 96, 128, X, oe, [])]
         m_1 = products(128, 0, g_1)
         z_1 = scaled("v", zs, Z, 128, 256, 64.0, g_1)
         m_2 = products(256, 4, g_2)
         z_2 = scaled("v", zs, Z, 256, 384, 64.0, g_2)
         g_b.append(pick("s", 0, S, B("dt"), B("le"), [d_cp, ("ae%d" % r, ne)]))
         r_1 = sums(128, 0, m_1, [z_1])
+        z_b = scaled("s", zs, Z, 0, 128, 64.0, g_b)
         r_2 = sums(256, 4, m_2, [z_2], (0, 1))
         m_b = products(0, 0, g_b)
-        z_b = scaled("s", zs, Z, 0, 128, 64.0, g_b)
         r_2 += sums(256, 4, m_2, [z_2], (2, 3))
         x_1 = scaled("v", Xn, xs, 128, 256, 0.015625, r_1)
-        x_2 = scaled("s", Xn, xs, 256, 384, 0.015625, r_2)
-        r_b = sums(0, 0, m_b, [z_b])
-        n_1 = state(128, [x_1])
-        n_2 = state(256, [x_2])
-        x_b = [scaled("v", Xn, xs, 0, 88, 0.015625, r_b), scaled("s", Xn, xs, 88, 128, 0.015625, r_b)]
-        n_b = state(0, x_b)
-        q_x, x_made, psum_free = [n_1, n_2, n_b], [x_1, x_2] + x_b, r_2 + r_b
+        state = {"banks_early": r_2}
+        if r + 1 < R:
+            x_2 = scaled("v", Xn, xs, 256, 384, 0.015625, r_2)
+            n_1 = packed(128, [x_1])
+            r_b = sums(0, 0, m_b, [z_b], (0,))
+            n_2 = packed(256, [x_2])
+            state["early"] = [n_1, n_2]
+            steps = places(r + 1, state)
+            next(steps)
+            r_b += sums(0, 0, m_b, [z_b], (1, 2, 3))
+        else:
+            steps = iter([None, None])
+            x_2 = scaled("s", Xn, xs, 256, 384, 0.015625, r_2)
+            r_b = sums(0, 0, m_b, [z_b])
+            n_1 = packed(128, [x_1])
+            n_2 = packed(256, [x_2])
+        state["banks_late"] = r_b
+        x_b = [act(Xn[:, b:512:4], xs[:, b:512:4], ACT.Copy, [r_b[b]], scale=0.015625) for b in (0, 1)]
+        x_b += [ts(Xn[:, b:512:4], xs[:, b:512:4], 0.015625, ALU.mult, deps=[r_b[b]]) for b in (2, 3)]
+        next(steps)
+        n_b = packed(0, x_b)
+        state["late"] = [n_b]
+        next(steps)
+        q_x, x_made = [n_1, n_2, n_b], [x_1, x_2] + x_b
 
     qn, sn = T["qx%d" % R], T["sx%d" % R]
+    e_f = act(T.ef[:], T["ec%d" % (R - 1)][:], ACT.Identity, [e_c], bias=float(H))
     for k, lo in enumerate((128, 256, 0)):
         y_k = mm(4 + k, 128, T.qv[:], T.sv[:], qn[:, lo:lo + 128], sn[:, lo:lo + 128], [late["qv"]] + r_2 + [q_x[k]])
         dma("y", T.oc[:, 4 * lo:4 * lo + 512], qn[:, lo:lo + 128].bitcast(dt.uint8), [q_x[k]], group="st")
@@ -491,6 +628,7 @@ def rank_program(g, core, T, topo):
             c_k = cp(T.yt[:, lo:lo + 128], bank(4 + k, 0, 128), [y_k])
     for k in range(4):
         dma("ys"[k % 2], T.osc[4 * k:4 * k + 4, :], sn[32 * k:32 * k + 4, :], q_x, group="st")
+    dma("y", T.el[:], T.ef[0:128:16, :], [e_f], group="st")
     dma("y", T.y[:, 0:128], T.yt[:, 0:128], [c_k], group="st")
     add(plan, "y", None, ["st"])
     add(plan, "g", None, [("sent", sends[0])])

from concourse.mybir import dt, AluOpType, ActivationFunctionType

ALU = AluOpType
ACT = ActivationFunctionType
C, S, R = 384, 96, 2
STEP = [2, 1]
NW = C // 16
E = 256
BY_SCALAR = [(14, 21), (9, 17)]
SUMS = [4, 8]
NT = NW // 4
BIG = 2.0 ** 40
FAR = 2.0 ** 96
KEY = 1024.0
H = C // 2
CUT = [0, H, C]
X4, U8, BF, F32, U16, I32 = "float8_e4m3fn_x4", "uint8", "bfloat16", "float32", "uint16", "int32"
WIDTH = [64 * a + 64 for a in range(NT)]
START = [sum(WIDTH[a + 1:]) for a in range(NT)]
WORDS = sum(WIDTH) + 64


def weights(r, a):
    return tuple(0.5 if BY_SCALAR[r][0] <= c < BY_SCALAR[r][1] else 1.0 for c in range(4 * a + 1, 4 * a + 5))


KINDS = sorted(set(weights(r, a) for r in range(R) for a in range(NT)), reverse=True)

SCRATCH = {
    "ps": ("psum", [128, 4096], F32),
    "ut": ("sbuf", [128, 512], BF), "vt": ("sbuf", [128, 512], BF),
    "qu": ("sbuf", [128, 128], X4), "su": ("sbuf", [128, 128], U8),
    "qur": ("sbuf", [128, 128], X4), "sur": ("sbuf", [128, 128], U8),
    "qv": ("sbuf", [128, 128], X4), "sv": ("sbuf", [128, 128], U8),
    "qw": ("sbuf", [128, 512], X4), "sw": ("sbuf", [128, 512], U8),
    "ones": ("sbuf", [128, 528], BF), "et": ("sbuf", [128, 528], BF),
    "qe": ("sbuf", [128, 512], X4), "se": ("sbuf", [128, 512], U8),
    "bw": ("sbuf", [128, 512 * len(KINDS)], BF),
    "qb": ("sbuf", [128, 128 * len(KINDS)], X4), "sq": ("sbuf", [128, 128 * len(KINDS)], U8),
    "ci": ("sbuf", [128, 64], I32), "cf": ("sbuf", [128, 64], F32), "cs": ("sbuf", [128, 160], BF),
    "cu": ("sbuf", [128, 96], U16),
    "wide": ("sbuf", [128, 4 * C], BF), "jr": ("sbuf", [128, C], BF), "jc": ("sbuf", [128, C], BF),
    "iall": ("sbuf", [128, C + 8], F32),
    "ft": ("sbuf", [128, 4 * WORDS], BF), "qf": ("sbuf", [128, WORDS], X4), "sf": ("sbuf", [128, WORDS], U8),
    "sg": ("sbuf", [128, NW * C], BF), "sb": ("sbuf", [128, NW * H], BF),
    "ef": ("sbuf", [128, C], F32), "yt": ("sbuf", [128, C], F32),
}
for _r in range(R + 1):
    SCRATCH["x%d" % _r] = ("sbuf", [128, 4 * C], BF)
    SCRATCH["qx%d" % _r] = ("sbuf", [128, C], X4)
    SCRATCH["sx%d" % _r] = ("sbuf", [128, C], U8)
for _r in range(R):
    for _n, _w, _d in (("lq", C, X4), ("ls", C, U8), ("li", NW, U16), ("le", NW, U16),
                       ("dt", 4 * C, BF), ("z", 4 * C, BF), ("zs", 4 * C, BF), ("xs", 4 * C, BF),
                       ("qz", C, X4), ("sz", C, U8),
                       ("pm", C, F32), ("pw", C, F32), ("ne", C, BF), ("hc", C, BF), ("acc", 96, F32),
                       ("oc_", C, BF), ("ec", C, BF), ("tab", 9 * C, BF), ("hs", 10 * C, BF),
                       ("ka", 10 * C, F32), ("kb", 9 * C, F32), ("tl", 3 * C, F32), ("pc", C, BF),
                       ("off", 12 * NW, U16), ("oe", 4 * NW, U16)):
        SCRATCH["%s%d" % (_n, _r)] = ("sbuf", [128, _w], _d)

POOLS = {"v": 40, "s": 40, "t": 40, "g": 12}
SEMAPHORES = ["%s%d" % (q, k) for q in POOLS for k in range(POOLS[q])] + ["d%d" % i for i in range(1, 8)] + ["sent"] + \
    ["%s%d" % (k, r) for k in ("aq", "ai", "ae") for r in range(R)]


def make_plan():
    return {"ops": [], "groups": {}}


def add(plan, queue, fn, deps=(), group=None, dma=False):
    ops = plan["ops"]
    ops.append({"q": queue, "fn": fn, "deps": [d for d in deps if d is not None], "group": group, "dma": dma})
    i = len(ops) - 1
    if group is not None:
        plan["groups"].setdefault(group, []).append(i)
        return group
    return i


def emit(plan, queues, sem):
    ops, groups = plan["ops"], plan["groups"]
    known = {q: {} for q in queues}
    past, waits, needed = [], [], set()
    for op in ops:
        want = {}
        for d in op["deps"]:
            if isinstance(d, tuple) or ops[groups[d][0] if d in groups else d]["dma"]:
                want[d] = 1
            else:
                for m in groups.get(d, [d]):
                    want[ops[m]["q"]] = max(want.get(ops[m]["q"], -1), m)
        mine, w = known[op["q"]], []
        for key, at in sorted(want.items(), key=lambda kv: -kv[1]):
            if mine.get(key, -1) >= at:
                continue
            w.append((key, at))
            needed.add(at if key in queues else key)
            mine[key] = at
            for m in ([at] if key in queues else [] if isinstance(key, tuple) else groups.get(key, [key])):
                for k2, at2 in past[m].items():
                    mine[k2] = max(mine.get(k2, -1), at2)
        waits.append(w)
        past.append(dict(mine))
    count, last, where = {}, {}, {}
    for i, op in enumerate(ops):
        q = queues[op["q"]]
        for key, at in waits[i]:
            q.wait_ge(*((sem[key[0]], key[1]) if isinstance(key, tuple) else where[at if key in queues else key]))
        if op["fn"] is None:
            continue
        ins = op["fn"]()
        if op["dma"]:
            key = i if op["group"] is None else op["group"]
            if key in needed:
                if key not in where:
                    count["d"] = count.get("d", 0) + 1
                    where[key] = (sem["d%d" % count["d"]], 16 * len(groups.get(key, [i])))
                ins.then_inc(where[key][0], 16)
        elif i in needed:
            pool = ["%s%d" % (op["q"], k) for k in range(POOLS[op["q"]])]
            name = [n for n in pool if last.get(n, -1) <= past[i].get(op["q"], -1)][0]
            last[name] = i
            count[name] = count.get(name, 0) + 1
            where[i] = (sem[name], count[name])
            ins.then_inc(where[i][0], 1)


def rank_program(g, core, T, topo):
    rank = T.rank_of(core)
    if rank is None:
        return
    plan = make_plan()
    V, A, PE = g.vector, g.scalar, g.tensor

    def v(fn, deps=(), group=None):
        return add(plan, "v", fn, deps, group)

    def s(fn, deps=(), group=None):
        return add(plan, "s", fn, deps, group)

    def pe(fn, deps=(), group=None):
        return add(plan, "t", fn, deps, group)

    def gp(fn, deps=(), group=None):
        return add(plan, "g", fn, deps, group)

    def dma(queue, out, in_, deps=(), group=None):
        eng = g.sync if queue == "y" else g.scalar
        return add(plan, queue, lambda: eng.dma_start(out, in_), deps, group, dma=True)

    def ts(out, in0, s1, op0, s2=None, op1=None, deps=(), group=None):
        if op1 is None:
            return v(lambda: V.tensor_scalar(out, in0, s1, None, op0), deps, group)
        return v(lambda: V.tensor_scalar(out, in0, s1, s2, op0, op1), deps, group)

    def tt(out, in0, in1, op, deps=(), group=None):
        return v(lambda: V.tensor_tensor(out, in0, in1, op), deps, group)

    def scan(out, d0, d1, init, op0, op1, deps=(), group=None):
        return v(lambda: V.tensor_tensor_scan(out, d0, d1, init, op0, op1), deps, group)

    def cp(out, in_, deps=(), group=None):
        return v(lambda: V.tensor_copy(out, in_), deps, group)

    def act(out, in_, func, deps=(), group=None, **kw):
        return s(lambda: A.activation(out, in_, func, **kw), deps, group)

    def quant(q, sc, in_, deps=(), group=None):
        return v(lambda: V.quantize_mx(q, sc, in_), deps, group)

    def mm(bank, n, lq, ls, rq, rs, deps=(), group=None, start=True, stop=True):
        return pe(lambda: PE.matmul_mx(T.ps[:, 512 * bank:512 * bank + n], lq, ls, rq, rs, start, stop), deps, group)

    def bank(b, lo, hi):
        return T.ps[:, 512 * b + lo:512 * b + hi]

    sends = [0]

    def remote(dst, out, in_, name, deps):
        rid, pid, ring = topo.addr(dst)
        sends[0] += len(topo.engines(core, dst))
        return gp(lambda: g.remote_dma(out, in_, T.sem[name], T.sem.sent, pid, rid, topo.mask(core, dst)), deps)

    ld_u = dma("s", T.ut[:], T.u[:])
    ld_x = [dma("y", T.x0[:, 0:4 * E], T.x[:, 0:4 * E]), dma("y", T.x0[:, 4 * E:4 * C], T.x[:, 4 * E:4 * C])]

    fl_ok = {"allow_small_or_imprecise_dtypes": True}
    ip = gp(lambda: g.iota(T.ci[:, 0:2], [[0, 2]], 0, 1))
    gp(lambda: g.iota(T.ci[:, 16:24], [[16, 8]], 0, 0), group="iu")
    iu = gp(lambda: g.iota(T.ci[:, 24:56], [[1, 8], [0, 4]], 0, 0), group="iu")
    it = gp(lambda: g.iota(T.cf[:, 0:NW + 1], [[1, NW + 1]], -1, 0, **fl_ok))
    c_jr = gp(lambda: g.iota(T.jr[:], [[0, NW], [1, 16]], 0, 0, **fl_ok))
    c_jc = gp(lambda: g.iota(T.jc[:], [[1, C]], -H, 0, **fl_ok))

    def col(k):
        return T.cf[:, k:k + 1]

    def small(k):
        return T.cs[:, 16 * k:16 * k + 16]

    def wide(k):
        return T.wide[:, C * k:C * k + C]

    blank = v(lambda: V.memset(T.ft[:, 4 * START[0]:4 * WORDS], 0.0))
    for a in range(1, NT):
        end = START[a] + WIDTH[a]
        zero = dma("y", T.ft[:, 4 * (end - 48):4 * end], T.ft[:, 4 * (WORDS - 48):4 * WORDS], [blank, ld_x[0]], group="zero")
    ld_w = dma("y", T.qw[:].bitcast(dt.uint8), T.wc[:], ld_x, group="ldw")
    dma("y", T.sw[:], T.ws[:], group="ldw")
    ld_v = dma("y", T.vt[:], T.v[:])

    less1, t16, t24 = T.cf[:, 0:16], T.cf[:, 1:17], T.cf[:, 1:NW + 1]
    qcol, gcol, rcol, hcol = col(32), col(33), col(34), col(35)
    sc16, scm, sc4, add4, big16, base = col(36), col(37), col(38), col(39), col(40), col(41)
    ts(T.ci[:, 4:5], T.ci[:, 0:1], 15, ALU.bitwise_and, deps=[ip], group="pi")
    pi = ts(T.ci[:, 5:6], T.ci[:, 0:1], 4, ALU.logical_shift_right, deps=[ip], group="pi")
    pf = cp(T.cf[:, 32:34], T.ci[:, 4:6], [pi])
    uo = cp(T.cu[:, 48:88], T.ci[:, 16:56], [iu])
    k_grp = ts(small(0), t16, gcol, ALU.is_equal, deps=[it, pf])
    late = {}
    q_u = quant(T.qu[:], T.su[:], T.ut[:], [ld_u])
    padded = quant(T.qf[:, WORDS - 128:WORDS], T.sf[:, WORDS - 128:WORDS], T.ft[:, 4 * (WORDS - 128):4 * WORDS], [blank])
    cp(T.qur[:].bitcast(dt.uint32), T.qu[:].bitcast(dt.uint32).indirect(T.cu[:, 48:56]), [uo, q_u], group="ur")
    c_bw = [act(T.bw[:, 0:512], small(0).indirect(T.cu[:, 56:88]), ACT.Copy, [uo, k_grp])]
    q_ur = act(T.sur[:], T.su[:].indirect(T.cu[:, 48:56]), ACT.Copy, [uo, q_u], group="ur")
    for k, w in list(enumerate(KINDS))[1:]:
        for t, step in ([(0, 1)] if len(set(w)) == 1 else [(t, 4) for t in range(4)]):
            made = act(T.bw[:, 512 * k + t:512 * k + 512:step], T.bw[:, t:512:step], ACT.Copy, [c_bw[0]], scale=w[t])
        c_bw.append(made)

    def adder(k):
        late["bd", k] = quant(T.qb[:, 128 * k:128 * k + 128], T.sq[:, 128 * k:128 * k + 128],
                              T.bw[:, 512 * k:512 * k + 512], [c_bw[k]])

    def unpacker(b):
        return lambda: late.update(qe=quant(T.qe[:, 128 * b:128 * b + 128], T.se[:, 128 * b:128 * b + 128],
                                            T.et[:, 3 - b:3 - b + 512], [late["et"]], group="qe"))

    gaps = [
        [lambda: ts(T.ci[:, 6:7], T.ci[:, 0:1], 3, ALU.bitwise_and, deps=[ip], group="pj"),
         lambda: ts(T.ci[:, 7:8], T.ci[:, 0:1], 2, ALU.logical_shift_right, 3, ALU.bitwise_and, deps=[ip], group="pj")],
        [lambda: late.update(pg=cp(T.cf[:, 34:36], T.ci[:, 6:8], ["pj"]))],
        [lambda: late.update(a4=ts(small(5), t16, hcol, ALU.is_gt, deps=[it, late["pg"]])),
         lambda: late.update(c4=ts(small(9), less1, hcol, ALU.is_equal, BIG, ALU.mult, [it, late["pg"]]))],
        [lambda: late.update(ro=ts(T.cu[:, NW:2 * NW], t24, 0.0, ALU.mult, rcol, ALU.add, [it, late["pg"]])),
         lambda: late.update(s4=ts(col(43), hcol, 3.0, ALU.is_equal, 1.0 / BIG, ALU.max, [late["pg"]]))],
        [unpacker(0)], [unpacker(1)], [unpacker(2)], [unpacker(3)],
        [lambda: late.update(qv=quant(T.qv[:], T.sv[:], T.vt[:], [ld_v]))],
    ]

    def gap():
        for make in (gaps.pop(0) if gaps else []):
            make()

    def places(r, state):
        mate = T.cores[rank ^ STEP[r]]
        qx, sx, pm, pw, nb, acc, hc, off = [T["%s%d" % (n, r)] for n in ("qx", "sx", "pm", "pw", "ne", "acc", "hc", "off")]
        ft, sb, sg = T.ft, T.sb, T.sg
        (S0, S1), K, turned = BY_SCALAR[r], SUMS[r], r > 0
        rows, within, signs, order = {}, {}, [], []

        def score(lo, hi):
            return bank(4, lo, hi) if hi <= E else bank(0, lo - E * turned, hi - E * turned)

        def own(lo, hi, made):
            return tt(pm[:, lo:hi], score(lo, hi), T.wide[:, lo:hi], ALU.add, [w_own, made])

        def hold(lo, hi, m):
            return scan(pw[:, lo:hi], T.wide[:, C + lo:C + hi], pm[:, lo:hi], 0.0, ALU.add, ALU.min, [w_new, m])

        def flags(c, lo, hi, step=4, first=0):
            at = 4 * START[(c - 1) // 4] + (c - 1) % 4
            return ft[:, at + 4 * lo + first:at + 4 * hi - 3:step]

        def mine(c):
            return pw[:, 16 * c + 15:16 * c + 16]

        def by_scalar(cs, deps):
            for c in cs:
                if c:
                    signs.append((c, act(sg[:, C * c:C * c + 16 * c], bank(5 if 16 * c <= E else 1, 0, 16 * c), ACT.Sign,
                                         deps, bias=mine(c), scale=-1.0)))
                if len(signs) == 2 or not c:
                    d, sign = signs.pop(0)
                    rows[d] = act(flags(d, 0, 16 * d), sg[:, C * d:C * d + 16 * d], ACT.Sign, [zero, sign], scale=-1.0,
                                  bias=-0.5 if turned and 16 * d >= E else 0.5, accum_out=acc[:, d:d + 1])

        def compare(cs, held):
            for c in cs:
                if 16 * c < E or not turned:
                    rows[c] = ts(flags(c, 0, 16 * c), score(0, 16 * c), mine(c), ALU.is_ge, 0.5, ALU.subtract, [zero, held])
                else:
                    ts(flags(c, 0, E), score(0, E), mine(c), ALU.is_gt, 0.5, ALU.subtract, [zero, held])
                    rows[c] = ts(flags(c, E, 16 * c), score(E, 16 * c), mine(c), ALU.is_ge, 0.5, ALU.subtract)

        def sixteens(lo, hi, held):
            rows[NW] = tt(flags(NW, lo, hi), score(lo, hi), pw[:, lo:hi], ALU.is_gt, [zero, held])
            return rows[NW]

        def runs(lo, hi, made):
            within[lo] = scan(nb[:, lo:hi], T.wide[:, lo:hi], flags(NW, lo, hi), 0.0, ALU.min, ALU.add, [made])

        def add_up(cs):
            for c in cs:
                scan(sb[:, H * c + H - 8 * c:H * c + H], flags(c, 0, 16 * c, 8), flags(c, 0, 16 * c, 8, 4),
                     nb[:, 16 * c + 15:16 * c + 16], ALU.add, ALU.add, [within[E * (16 * c >= E)], rows[c]], group="cnt%d" % r)

        def add_up_short():
            for c in range(K, 0, -1):
                rows[c] = act(sg[:, C * c:C * c + 16 * c], flags(c, 0, 16 * c), ACT.Copy, [rows[c]], scale=2.0,
                              accum_out=acc[:, c:c + 1])

        def pack(tiles):
            lo, hi = START[tiles[0]], START[tiles[-1]] + WIDTH[tiles[-1]]
            done = quant(T.qf[:, lo:hi], T.sf[:, lo:hi], ft[:, 4 * lo:4 * hi],
                         [padded] + [rows[c] for a in tiles for c in range(4 * a + 1, 4 * a + 5)])
            for a in tiles:
                k, n = 128 * KINDS.index(weights(r, a)), max(128, WIDTH[a])
                order.append(a)
                mm(6, n, T.qb[:, k:k + 128], T.sq[:, k:k + 128], T.qf[:, START[a]:START[a] + n],
                   T.sf[:, START[a]:START[a] + n], [late["bd", k // 128], done],
                   group="down%d" % r, start=len(order) == 1, stop=len(order) == NT)

        def send():
            remote(mate, T["ls%d" % r][:], sx[:], "aq%d" % r, state["early"] + state["late"])

        at = (C - E) * turned
        p_v = mm(4, E, T.qur[:], T.sur[:], qx[:, at:at + E], sx[:, at:at + E], [q_ur] + state["banks_early"] + state["early"])
        p_s = mm(5, E, T.qur[:], T.sur[:], qx[:, at:at + E], sx[:, at:at + E])
        none = act(acc[:, 0:1], col(1), ACT.Copy, [it], scale=0.0)
        yield
        if not turned:
            yield
            p_l = mm(0, C, T.qur[:], T.sur[:], qx[:], sx[:], state["late"])
            p_a = mm(1, C, T.qur[:], T.sur[:], qx[:], sx[:])
            send()
            made = [own(16 * S0, E, p_v), own(0, 16 * S0, p_v)]
            pw_s, pw_e = hold(16 * S0, E, made[0]), hold(0, 16 * S0, made[1])
            by_scalar([15, 14], [p_s, pw_s])
            m_l = own(E, C, p_l)
            f_e = sixteens(0, E, pw_e)
            pw_l = hold(E, C, m_l)
            by_scalar([20, 19, 18, 17, 16, None], [p_a, pw_l])
            next(state["soon"])
            runs(0, E, f_e)
            compare([23, 22, 21], pw_l)
            f_l = sixteens(E, C, pw_l)
            compare([13], pw_e)
            runs(E, C, f_l)
            pack([5])
            compare(range(8, 0, -1), pw_e)
            next(state["soon"])
            pack([1, 0])
            add_up_short()
            compare([12, 11, 10], pw_e)
            pack([4])
            compare([9], pw_e)
            pack([3])
            pack([2])
            last = [23, 22, 21] + list(range(S0 - 1, K, -1))
        else:
            made = [own(16 * 13, E, p_v), own(0, 16 * 13, p_v)]
            yield
            p_l = mm(0, C - E, T.qur[:], T.sur[:], qx[:, 0:C - E], sx[:, 0:C - E], state["banks_late"] + state["late"])
            send()
            pw_s, pw_e = hold(16 * 13, E, made[0]), hold(0, 16 * 13, made[1])
            yield
            by_scalar([15, 14, 13], [p_s, pw_s])
            f_e = sixteens(0, E, pw_e)
            m_l = own(E, C, p_l)
            compare(range(S0 - 1, 3, -1), pw_e)
            pw_l = hold(E, C, m_l)
            by_scalar([16] + list(range(12, S0 - 1, -1)) + [None], [pw_l])
            compare([3, 2, 1], pw_e)
            runs(0, E, f_e)
            compare([23, 22, 21], pw_l)
            f_l = sixteens(E, C, pw_l)
            compare([20], pw_l)
            runs(E, C, f_l)
            pack([5])
            pack([1, 0])
            pack([3])
            compare([19, 18, 17], pw_l)
            pack([2])
            pack([4])
            add_up_short()
            last = list(range(NW - 1, S1 - 1, -1)) + list(range(S0 - 1, K, -1))
        yield
        spans = [(0, S1)] if K + 1 == S0 else [(S0, S1), (0, K + 1)]
        rows[0] = none
        add_up(last[:-3])
        by_s = [ts(acc[:, 64 + lo:64 + hi], acc[:, lo:hi], 0.5, ALU.mult, deps=[rows[c] for c in range(lo, hi)])
                for lo, hi in spans]
        add_up(last[-3:])
        for k, (lo, hi) in enumerate(spans):
            tt(sb[:, H * lo + H - 1:H * hi:H], acc[:, 64 + lo:64 + hi], nb[:, 16 * lo + 15:16 * hi:16], ALU.add,
               list(within.values()) + [by_s[k]], group="cnt%d" % r)
        h_c = [scan(hc[:, 0:E], T.wide[:, 2 * C:2 * C + E], bank(6, 0, E), 0.0, ALU.mult, ALU.add, [late["w16"], "down%d" % r])]
        along = ts(acc[:, 32:32 + NW], sb[:, H - 1:H * NW:H], big16, ALU.mult, deps=[late["big"], "cnt%d" % r])
        h_c.append(scan(hc[:, E:C], T.wide[:, 2 * C + E:3 * C], bank(6, E, C), 0.0, ALU.mult, ALU.add))
        both = [tt(acc[:, (lo + at) % C // 16:(lo + at) % C // 16 + (hi - lo) // 16], acc[:, 32 + lo // 16:32 + hi // 16],
                   hc[:, lo + 15:hi:16], ALU.subtract, [along, h_c[k]]) for k, (lo, hi) in enumerate(((0, E), (E, C)))]
        state["places"] = ts(off[:, 0:NW], acc[:, 0:NW], sc16, ALU.mult, base, ALU.add, [late["sc"], late["base"]] + both)
        remote(mate, T["li%d" % r][:], off[:, 0:NW], "ai%d" % r, [state["places"]])
        remote(mate, T["lq%d" % r][:].bitcast(dt.uint8), qx[:].bitcast(dt.uint8), "aq%d" % r, [])
        yield

    state = {"banks_early": [], "banks_late": [], "late": []}
    steps = places(0, state)
    state["early"] = [quant(T.qx0[:, 0:E], T.sx0[:, 0:E], T.x0[:, 0:4 * E], [ld_x[0]])]
    next(steps)
    w_own = ts(wide(0), T.jr[:], qcol, ALU.not_equal, FAR, ALU.mult, [pf, c_jr])
    q_l = quant(T.qx0[:, E:C], T.sx0[:, E:C], T.x0[:, 4 * E:4 * C], [ld_x[1]])
    w_new = ts(wide(1), T.jr[:], 0.0, ALU.is_equal, FAR, ALU.mult, [c_jr])
    adder(0)
    k_a16 = ts(small(2), t16, qcol, ALU.is_gt, deps=[it, pf])
    k_c16 = ts(small(8), less1, qcol, ALU.is_equal, BIG, ALU.mult, [it, pf])
    next(steps)
    state["late"] = [q_l]

    def soon():
        late["qo"] = ts(T.cu[:, 0:NW], t24, 0.0, ALU.mult, qcol, ALU.add, [it, pf])
        late["h16"] = tt(small(3), small(8), small(2), ALU.max, [k_a16, k_c16])
        yield
        late["sc"] = ts(sc16, qcol, 15.0, ALU.is_equal, 1.0 / BIG, ALU.max, [pf])
        late["up"] = ts(col(42), qcol, 15.0, ALU.is_lt, BIG, ALU.mult, [pf])
        for k in range(1, len(KINDS)):
            adder(k)
        yield

    state["soon"] = soon()
    x_made = list(ld_x)

    for r in range(R):
        mate = T.cores[rank ^ STEP[r]]
        ne = len(topo.engines(mate, core))

        def B(name, r=r):
            return T["%s%d" % (name, r)]

        X, qx, sx = B("x"), B("qx"), B("sx")
        off = B("off")

        def offs(k):
            return off[:, NW * k:NW * k + NW]

        def part(buf, k):
            return buf[:, C * k:C * k + C]

        next(steps)
        if r == 0:
            late["w16"] = act(wide(2), small(3).indirect(T.cu[:, 0:NW]), ACT.Copy, [late["qo"], late["h16"]])
            late["big"] = act(big16, col(42), ACT.Identity, [late["up"]], bias=1.0)
            late["base"] = act(base, qcol, ACT.Identity, [pf], bias=H - 8.0)
        fill_o = act(B("oc_")[:], T.jr[:], ACT.Copy, [c_jr], scale=0.0)
        next(steps)
        if r == 0:
            one = gp(lambda: g.iota(T.ones[:], [[0, 528]], 1, 0, **fl_ok))
            late["et"] = gp(lambda: g.affine_select(T.et[:], T.ones[:], [[-1, 528]], ALU.is_equal, 0.0, 3, 4), [one])
            c_i = gp(lambda: g.iota(T.iall[:], [[int(KEY), C + 8]], -int(KEY), 0, **fl_ok))
        o_c = cp(B("oc_")[:].indirect(offs(0)), T.jc[:], [c_jc, fill_o, state["places"]])
        fill_e = act(B("ec")[:], T.jr[:], ACT.Copy, scale=0.0)

        tab, hs, ka, kb = B("tab"), B("hs"), B("ka"), B("kb")
        came = ("ai%d" % r, ne)

        def half(buf, k, h):
            return buf[:, C * k + CUT[h]:C * k + CUT[h + 1]]

        def list_half(tile, k, h):
            return tile[:, NW * k + CUT[h] // 16:NW * k + CUT[h + 1] // 16]

        def wrap(src, k, via, to, made):
            lifted = [scan(half(hs, via, h), half(T.wide, 2, h), half(src, k, h), 0.0, ALU.mult, ALU.add, [made[h]])
                      for h in range(2)]
            return [ts(list_half(off, to, h), hs[:, C * via + CUT[h] + 15:C * via + CUT[h + 1]:16], sc16, ALU.mult,
                       float(H), ALU.add, [lifted[h]]) for h in range(2)]

        def third(buf, k, h):
            return buf[:, C * k + 128 * h:C * k + 128 * h + 128]

        def list_third(tile, k, h):
            return tile[:, NW * k + 8 * h:NW * k + 8 * h + 8]

        def key(k, h, deps):
            if k == 0:
                return ts(third(ka, 0, h), B("oc_")[:].indirect(list_third(B("li"), 0, h)), KEY, ALU.mult, KEY * H + C, ALU.add,
                          [came, o_c])
            return tt(third(ka, k, h), part(ka, k - 1).indirect(list_third(off, k, h)), third(kb, k - 1, h), ALU.min, deps)

        def lift(k, h):
            return scan(third(hs, k, h), third(T.wide, 2, h), third(tab, k, h), 0.0, ALU.mult, ALU.add, [t_k[h]])

        def listed_as(k, h, lifted):
            return ts(list_third(off, k + 1, h), hs[:, C * k + 128 * h + 15:C * k + 128 * h + 128:16], sc16, ALU.mult,
                      float(H), ALU.add, [lifted])

        a_k = [key(0, 0, []), key(0, 1, [])]
        t_k, o_k, last = [came, o_c], [None] * 3, []
        for k in range(8):
            lst = off if k else B("li")
            t_k = [act(third(tab, k, h), (part(tab, k - 1) if k else B("oc_")[:]).indirect(list_third(lst, k, h)), ACT.Copy,
                       t_k + [o_k[h]]) for h in range(3)]
            s_0 = lift(k, 0)
            a_k.append(key(k, 2, last))
            b_k = [act(third(kb, k, h), third(ka, k, h), ACT.Identity, [a_k[h]], bias=-float(2 ** k)) for h in range(3)]
            s_1 = lift(k, 1)
            o_k = [listed_as(k, 0, s_0)]
            gap()
            s_2 = lift(k, 2)
            o_k.append(listed_as(k, 1, s_1))
            a_n = [key(k + 1, 0, a_k + [o_k[0], b_k[0]])]
            o_k.append(listed_as(k, 2, s_2))
            a_n.append(key(k + 1, 1, [o_k[1], b_k[1]]))
            a_k, last = a_n, [o_k[2], b_k[2]]
        b_last = act(part(kb, 8), part(ka, 7), ACT.Identity, b_k, bias=-256.0)
        a_k.append(key(8, 2, last))
        if r == 0:
            late["h4"] = tt(small(4), small(9), small(5), ALU.max, [late["a4"], late["c4"]])
        a_k = [tt(half(ka, 9, h), part(ka, 8).indirect(list_half(off, 8, h)), half(kb, 8, h), ALU.min, [b_last] + a_k)
               for h in range(2)]
        if r == 0:
            w_h4 = act(wide(3), small(4).indirect(T.cu[:, NW:2 * NW]), ACT.Copy, [late["ro"], late["h4"]])
            k_scm = act(scm, sc16, ACT.Copy, scale=1.0 / KEY)
            k_sc4 = act(sc4, col(43), ACT.Copy, [late["s4"]], scale=4.0)
            k_add4 = act(add4, rcol, ACT.Identity, [late["pg"]], bias=4.0 * H)
        for b, at in enumerate((1, 2, 3, 7)):
            d_mm = mm(at, C, T.qe[:, 128 * b:128 * b + 128], T.se[:, 128 * b:128 * b + 128], B("lq")[:], B("ls")[:],
                      [late["qe"], ("aq%d" % r, 2 * ne)] + state["banks_early"] + state["banks_late"])
            d_cp = act(B("dt")[:, b:4 * C:4], bank(at, 0, C), ACT.Copy, [d_mm], group="dcp%d" % r)
        tl, pc, oe = B("tl"), B("pc"), B("oe")
        top, h_m = [], []
        for h in range(2):
            top.append(scan(half(tl, 1, h), half(ka, 9, h), T.iall[:, 1 + CUT[h]:1 + CUT[h + 1]], -1.0e6, ALU.max, ALU.max,
                            [c_i, a_k[h]]))
            h_m.append(scan(half(tl, 0, h), half(T.wide, 2, h), half(ka, 9, h), 0.0, ALU.mult, ALU.add, [a_k[h]]))
        m_w = [ts(list_half(off, 9, 0), tl[:, 15:CUT[1]:16], scm, ALU.mult, deps=[k_scm, h_m[0]])]
        ends = scan(part(tl, 2), part(tl, 1), T.iall[:, 0:C], -KEY - H, ALU.add, ALU.subtract, top)
        m_w.append(ts(list_half(off, 9, 1), tl[:, CUT[1] + 15:C:16], scm, ALU.mult, deps=[h_m[1]]))
        pos = [tt(half(pc, 0, h), part(tl, 2).indirect(list_half(off, 9, h)), half(ka, 9, h), ALU.subtract, [m_w[h], ends])
               for h in range(2)]
        o_p = wrap(pc, 0, 8, 10, pos)
        e_c = cp(B("ec")[:].indirect(offs(10)), T.jc[:], [fill_e] + o_p)
        cuts = [(0, 128), (128, C)]
        h_e = [scan(hs[:, 9 * C + lo:9 * C + hi], T.wide[:, 3 * C + lo:3 * C + hi], B("ec")[:, lo:hi], 0.0, ALU.mult, ALU.add,
                    [w_h4, e_c]) for lo, hi in cuts]
        o_e = [ts(oe[:, lo // 4:hi // 4], hs[:, 9 * C + lo + 3:9 * C + hi:4], sc4, ALU.mult, add4, ALU.add,
                  [k_sc4, k_add4, h_e[k]]) for k, (lo, hi) in enumerate(cuts)]
        remote(mate, B("le")[:], oe[:, 0:NW], "ae%d" % r, [o_e[0]])

        Z, zs, xs, qz, sz = B("z"), B("zs"), B("xs"), B("qz"), B("sz")
        Xn, qn, sn = T["x%d" % (r + 1)], T["qx%d" % (r + 1)], T["sx%d" % (r + 1)]
        free = [[] for b in range(8)]

        def pick(by, lo, hi, src, lst, deps):
            out, in_ = Z[:, 4 * lo:4 * hi], src[:].indirect(lst[:, lo // 4:hi // 4])
            return cp(out, in_, deps) if by == "v" else act(out, in_, ACT.Copy, deps)

        def scaled(by, out, in_, lo, hi, c, deps):
            if by == "v":
                return ts(out[:, 4 * lo:4 * hi], in_[:, 4 * lo:4 * hi], c, ALU.mult, deps=deps)
            return act(out[:, 4 * lo:4 * hi], in_[:, 4 * lo:4 * hi], ACT.Copy, deps, scale=c)

        def products(lo, first, deps):
            done = quant(qz[:, lo:lo + 128], sz[:, lo:lo + 128], Z[:, 4 * lo:4 * lo + 512], deps)
            return [mm(first + b, 128, T.qw[:, 128 * b:128 * b + 128], T.sw[:, 128 * b:128 * b + 128], qz[:, lo:lo + 128],
                       sz[:, lo:lo + 128], [ld_w, d_cp] + free[first + b] + [done]) for b in range(4)]

        def sums(lo, first, made, deps, bs=range(4)):
            for b in bs:
                free[first + b] = [tt(xs[:, 4 * lo + b:4 * lo + 512:4], bank(first + b, 0, 128),
                                      zs[:, 4 * lo + b:4 * lo + 512:4], ALU.add, deps + [made[b]])]
            return [free[first + b][0] for b in bs]

        def packed(lo, deps):
            return quant(qn[:, lo:lo + 128], sn[:, lo:lo + 128], Xn[:, 4 * lo:4 * lo + 512], deps)

        listed = x_made + [o_e[1]]
        g_1 = [pick("v", 128, 192, X, oe, listed), pick("s", 192, 256, X, oe, listed)]
        g_2 = [pick("v", 256, 304, X, oe, listed), pick("s", 304, 384, X, oe, listed)]
        g_b = [pick("s", 96, 128, X, oe, [])]
        m_1 = products(128, 0, g_1)
        z_1 = scaled("v", zs, Z, 128, 256, 64.0, g_1)
        m_2 = products(256, 4, g_2)
        z_2 = scaled("v", zs, Z, 256, 384, 64.0, g_2)
        g_b.append(pick("s", 0, S, B("dt"), B("le"), [d_cp, ("ae%d" % r, ne)]))
        r_1 = sums(128, 0, m_1, [z_1])
        z_b = scaled("s", zs, Z, 0, 128, 64.0, g_b)
        r_2 = sums(256, 4, m_2, [z_2], (0, 1))
        m_b = products(0, 0, g_b)
        r_2 += sums(256, 4, m_2, [z_2], (2, 3))
        x_1 = scaled("v", Xn, xs, 128, 256, 0.015625, r_1)
        state = {"banks_early": r_2}
        if r + 1 < R:
            x_2 = scaled("v", Xn, xs, 256, 384, 0.015625, r_2)
            n_1 = packed(128, [x_1])
            r_b = sums(0, 0, m_b, [z_b], (0,))
            n_2 = packed(256, [x_2])
            state["early"] = [n_1, n_2]
            steps = places(r + 1, state)
            next(steps)
            r_b += sums(0, 0, m_b, [z_b], (1, 2, 3))
        else:
            steps = iter([None, None])
            x_2 = scaled("s", Xn, xs, 256, 384, 0.015625, r_2)
            r_b = sums(0, 0, m_b, [z_b])
            n_1 = packed(128, [x_1])
            n_2 = packed(256, [x_2])
        state["banks_late"] = r_b
        x_b = [act(Xn[:, b:512:4], xs[:, b:512:4], ACT.Copy, [r_b[b]], scale=0.015625) for b in (0, 1)]
        x_b += [ts(Xn[:, b:512:4], xs[:, b:512:4], 0.015625, ALU.mult, deps=[r_b[b]]) for b in (2, 3)]
        next(steps)
        n_b = packed(0, x_b)
        state["late"] = [n_b]
        next(steps)
        q_x, x_made = [n_1, n_2, n_b], [x_1, x_2] + x_b

    qn, sn = T["qx%d" % R], T["sx%d" % R]
    e_f = act(T.ef[:], T["ec%d" % (R - 1)][:], ACT.Identity, [e_c], bias=float(H))
    for k, lo in enumerate((128, 256, 0)):
        y_k = mm(4 + k, 128, T.qv[:], T.sv[:], qn[:, lo:lo + 128], sn[:, lo:lo + 128], [late["qv"]] + r_2 + [q_x[k]])
        dma("y", T.oc[:, 4 * lo:4 * lo + 512], qn[:, lo:lo + 128].bitcast(dt.uint8), [q_x[k]], group="st")
        if lo:
            c_k = act(T.yt[:, lo:lo + 128], bank(4 + k, 0, 128), ACT.Copy, [y_k], group="ya")
        else:
            dma("s", T.y[:, 128:C], T.yt[:, 128:C], [c_k], group="st")
            c_k = cp(T.yt[:, lo:lo + 128], bank(4 + k, 0, 128), [y_k])
    for k in range(4):
        dma("ys"[k % 2], T.osc[4 * k:4 * k + 4, :], sn[32 * k:32 * k + 4, :], q_x, group="st")
    dma("y", T.el[:], T.ef[0:128:16, :], [e_f], group="st")
    dma("y", T.y[:, 0:128], T.yt[:, 0:128], [c_k], group="st")
    add(plan, "y", None, ["st"])
    add(plan, "g", None, [("sent", sends[0])])
    emit(plan, {"v": V, "s": A, "t": PE, "g": g, "y": g.sync}, T.sem)
